import numpy as np, ml_dtypes
CORES = [16,18,20,22]
N = 4
import mx_ref
BF = ml_dtypes.bfloat16
def gentries(a):
    return np.ascontiguousarray(a.reshape(8, 16, -1).transpose(0, 2, 1)).reshape(8, -1)
def gtable(e):
    e = np.asarray(e); return np.ascontiguousarray(e.reshape(8, -1, 16).transpose(0, 2, 1)).reshape(128, -1).astype(np.int32)
def gcols(t, e):
    v = np.concatenate([t.reshape(8, 16, -1, 4), np.zeros((8, 16, 1, 4), BF)], axis=2)
    return np.ascontiguousarray(np.stack([v[g][:, e[g]] for g in range(8)])).reshape(128, -1)
def tile(rs):
    return np.stack(rs, axis=2).reshape(128, -1).astype(BF)
def cut(t, i, w=512):
    return t[:, w * i:w * i + w]
def pick(q, e):
    c = np.concatenate([q[0].reshape(128, -1, 4), np.zeros((128, 1, 4), np.uint8)], axis=1); s = np.concatenate([q[1], np.ones((16, 1), np.uint8)], axis=1)
    return (np.ascontiguousarray(c[:, e].reshape(128, -1)), np.ascontiguousarray(s[:, e]))
def join(*qs):
    return (np.concatenate([q[0] for q in qs], axis=1), np.concatenate([q[1] for q in qs], axis=1))
def put(q, e, v):
    c, s = q[0].reshape(128, -1, 4).copy(), q[1].copy(); c[:, e] = v[0].reshape(128, -1, 4); s[:, e] = v[1]
    return (c.reshape(128, -1), s)
def pk(c, s):
    return (np.ascontiguousarray(c), mx_ref.live(s))
def emit(q):
    return q[0], q[1]
def packed(v, rng):
    q = [mx_ref.quantize(np.ascontiguousarray(v[r])) for r in range(N)]
    return np.stack([a for a, b in q]), np.stack([mx_ref.plane(b, rng) for a, b in q])
def values_of_codes():
    e, c = np.zeros((128, 128, 4), np.float32), np.zeros((128, 2, 4), np.uint8)
    e[np.arange(128), np.arange(128), 0] = 1
    c[:127, :, 0] = np.arange(256).reshape(2, 128).T[:127]
    return mx_ref.matmul(mx_ref.quantize(e.reshape(128, 512).astype(BF)), (c.reshape(128, 8), np.full((16, 2), 127, np.uint8))).T.reshape(-1).astype(np.float64)
CODE_VALUE, SCALE_VALUE = values_of_codes(), 2.0 ** (np.arange(256) - 127.0)
def decode(q):
    return (CODE_VALUE[q[0]].reshape(16, 8, -1, 4) * SCALE_VALUE[q[1]][:, None, :, None] + 0.0).reshape(128, -1).astype(np.float32)
def f(rng, *shape):
    return mx_ref.flush((rng.standard_normal(shape, dtype=np.float32) * np.exp2(rng.integers(-2, 3, shape[:-1] + (1,)))).astype(BF))
def wide(rng, *shape, cols=0):
    v = rng.standard_normal(shape, dtype=np.float32) * np.exp2(rng.integers(-12, 13, shape)).astype(np.float32)
    if cols: v *= np.repeat(np.exp2(rng.integers(-cols, cols + 1, shape[:-2] + (1, shape[-1] // 4))) * (rng.random(shape[:-2] + (1, shape[-1] // 4)) > 0.0625), 4, axis=-1).astype(np.float32)
    return mx_ref.flush(v.astype(BF))
C, K, A, R = 512, 192, 448, 3
def big(v):
    v = v.astype(np.float32)
    v[np.abs(v) < np.float32(2.0 ** -16)] = 0
    return v.astype(BF)
def numbers_of(rng):
    return {"x": big(f(rng, N, 128, 4 * C)), "u": np.array(f(rng, N, 128, 512)), "v": np.array(f(rng, N, 128, 512))}
def weights(rng, w):
    c, p = packed(w, rng)
    return {"wc": c, "ws": p}
def still(rng):
    w = np.zeros((N, 128, 4, 128, 4), np.float32)
    i = np.arange(128)
    for b in range(4): w[:, i, b, i, b] = 32
    return weights(rng, w.reshape(N, 128, 2048).astype(BF))
def clauses(rng):
    return rng.integers(0, C + K, (N, 8, A, 4))
def stored(l):
    return {"cl": np.stack([gtable(e) for e in l])}
def signs(rng):
    return np.stack([rng.permutation(8) % 2 * 2.0 - 1.0 for r in range(N)])
def setup_inputs(rng):
    return {**numbers_of(rng), **stored(clauses(rng)), **weights(rng, f(rng, N, 128, 2048))}
def setup_inputs_signs(rng):
    d = numbers_of(rng)
    o = rng.permutation(N)
    kinds = np.array([[0, 0, -1, -2, 1, 1, 1, 2], [0, 0, 0, -1, -1, -2, 1, 2], [0, -1, -1, -2, -2, -2, -1, -1], [1, 1, 1, 1, 2, 2, 1, 1]])
    small = rng.permutation(N) % 2 == 0
    x = d["x"].reshape(N, 8, 16, C, 4)
    u = d["u"].reshape(N, 128, 128, 4)
    x[:, :, :8] = 0
    u[:, :, ::16] = 0
    for r in range(N):
        i = rng.permuted(np.tile(np.arange(C) % 8, (8, 1)), axis=1)
        size = 2.0 ** -30 if small[r] else 1.0
        x[r, :, 0, :, 0] = ((12 + kinds[o[r] % 4][i]) * size).astype(np.float32).astype(BF)
        x[r, :, 0, :, 1] = 12 * size
        for h in range(0, 128, 16):
            u[r, h, h, 0] = size
            u[r, h, h, 1] = -size
    return {"x": x.reshape(N, 128, 4 * C), "u": u.reshape(N, 128, 512), "v": d["v"], **stored(clauses(rng)), **still(rng)}
def setup_inputs_near(rng):
    d = numbers_of(rng)
    x = d["x"].astype(np.float32).reshape(N, 8, 16, C, 4)
    s = np.minimum((np.arange(C) + 1) // 2, 255)
    g = ((s[:, None] >> np.arange(8)) & 1) * np.exp2(np.arange(8) - 23.0)
    x[:, :, 0] = 0
    x[:, :, 0, :, 0] = signs(rng)[:, :, None]
    x[:, :, 8] = g[:, :4]
    x[:, :, 9] = g[:, 4:]
    x[:, :, 10:] = rng.integers(4, 8, (N, 8, 6, C, 4)) * rng.choice([-1.0, 1.0], (N, 8, 6, C, 4)) * 2.0 ** -20
    u = d["u"].reshape(N, 128, 128, 4)
    k = np.where(rng.permutation(N) < N // 2, 2.0 ** -30, 1.0).astype(np.float32).astype(BF)
    u[:, :, ::16] = 0
    for h in range(0, 128, 16):
        u[:, h, h, 0] = k
        u[:, h + 8:h + 10, h] = k[:, None, None]
    return {"x": x.reshape(N, 128, 4 * C).astype(BF), "u": u.reshape(N, 128, 512), "v": d["v"], **stored(clauses(rng)), **still(rng)}
def setup_inputs_huge(rng):
    d = numbers_of(rng)
    x = 2.0 ** 30 * (0.8 + 0.2 * rng.random((N, 128, C, 4)))
    c = np.stack([rng.permutation(C) % 2 * 2.0 - 1.0 for r in range(N)])
    o = rng.permutation(N)
    c[o < N // 2] = 1
    for r in range(N):
        if o[r] >= N - N // 4: c[r] = np.where(np.arange(C) % 4 == rng.integers(4), 1.0, -1.0)
    x *= c[:, None, :, None]
    u = d["u"].reshape(N, 128, 128, 4)
    a = 2.0 ** 30 * (1 - 0.1 * rng.random((N, 128, 8, 4))) * signs(rng)[:, None, :, None]
    u[:, :, ::16] = a.astype(np.float32).astype(BF)
    return {"x": x.astype(np.float32).reshape(N, 128, 4 * C).astype(BF), "u": u.reshape(N, 128, 512), "v": d["v"], **stored(clauses(rng)), **still(rng)}
def setup_inputs_lists(rng):
    d = numbers_of(rng)
    l = clauses(rng)
    o = rng.permutation(N)
    for r in range(N):
        if o[r] % 4 == 0: l[r] = C + (np.argsort(rng.random((8, A)), axis=1) % K)[:, :, None]
        if o[r] % 4 == 1: l[r] = rng.integers(0, C, (8, A, 4))
        if o[r] % 4 == 2: l[r] = C + rng.integers(0, K, (8, 1, 1))
        if o[r] % 4 == 3:
            l[r, :, :256] = rng.integers(0, C, (8, 256, 4))
            l[r, :, 256:] = rng.integers(C, C + K, (8, A - 256, 4))
    return {**d, **stored(l), **weights(rng, f(rng, N, 128, 2048))}
def setup_inputs_spread(rng):
    d = setup_inputs(rng)
    d["x"] = big(wide(rng, N, 128, 4 * C, cols=6))
    return d
def check_inputs(d):
    b = []
    for k in ("x", "u", "v"):
        a = np.abs(d[k].astype(np.float32))
        if not (np.isfinite(a).all() and ((a == 0) | (a >= 2.0 ** -30) & (a <= 2.0 ** 30)).all()): b.append("a value of " + k)
    if ((d["cl"] < 0) | (d["cl"] >= C + K)).any(): b.append("an entry of cl")
    return b
def mean(a, b):
    return ((a.astype(np.float32) + b.astype(np.float32)) * np.float32(0.5)).astype(BF)
def reference(x, u, v, cl, wc, ws):
    qu = [mx_ref.quantize(u[r]) for r in range(N)]
    lay = [pk(wc[r], ws[r]) for r in range(N)]
    lit = [gentries(cl[r]).reshape(8, A, 4).astype(np.int64) for r in range(N)]
    now = [x[r] for r in range(N)]
    cur = [np.zeros((8, A), np.int64) for r in range(N)]
    for t in range(R):
        own, e, sent, back = [], [], [], []
        for r in range(N):
            own.append(mx_ref.matmul(qu[r], mx_ref.quantize(now[r]))[::16] + np.float32(0.0))
            e.append(np.argsort(-own[r], axis=1, kind="stable")[:, :K])
            sent.append(mx_ref.quantize(gcols(now[r], e[r])))
        came = decode(join(*sent)).astype(BF)
        for r in range(N):
            p = (r - 1) % N
            place = np.concatenate([now[r], cut(came, p, 4 * K)], axis=1)
            yes = np.concatenate([own[r], mx_ref.matmul(qu[r], sent[p])[::16]], axis=1) > 0
            named = np.stack([yes[g][lit[r][g]] for g in range(8)])
            turn = (cur[r][:, :, None] + np.arange(4)) % 4
            cur[r] = (cur[r] + np.argmax(np.take_along_axis(named, turn, axis=2), axis=2)) % 4
            one = np.take_along_axis(lit[r], cur[r][:, :, None], axis=2)[:, :, 0]
            two = np.take_along_axis(lit[r], (cur[r][:, :, None] + 1) % 4, axis=2)[:, :, 0]
            q = mx_ref.quantize(mean(gcols(place, one), gcols(place, two)))
            h = tile([mx_ref.matmul(pick(lay[r], np.arange(128 * b, 128 * b + 128)), q) * np.float32(0.03125) for b in range(4)])
            first = np.full((8, C + K), -1)
            for j in range(A - 1, -1, -1): first[np.arange(8), one[:, j]] = j
            back.append(mx_ref.quantize(gcols(h, first[:, C:])))
        home = decode(join(*back)).astype(BF)
        for r in range(N):
            new = now[r].copy().reshape(8, 16, C, 4)
            got = cut(home, (r + 1) % N, 4 * K).reshape(8, 16, K, 4)
            for g in range(8): new[g][:, e[r][g]] = mean(new[g][:, e[r][g]], got[g])
            now[r] = new.reshape(128, 4 * C)
    y, ow = np.zeros((N, 128, C), np.float32), np.zeros((N, 8, A), np.float32)
    oc, osc = np.zeros((N, 128, 4 * C), np.uint8), np.zeros((N, 16, C), np.uint8)
    for r in range(N):
        q = mx_ref.quantize(now[r])
        y[r] = mx_ref.matmul(mx_ref.quantize(v[r]), q)
        ow[r] = cur[r]
        oc[r], osc[r] = emit(q)
    return {"y": y, "ow": ow, "oc": oc, "osc": osc}

@@ -1,0 +1,590 @@
+from concourse.mybir import dt, AluOpType, ActivationFunctionType
+
+ALU = AluOpType
+ACT = ActivationFunctionType
+
+C, K, A, R = 512, 192, 448, 3
+PL = C + K
+HW = 784
+NONE_AT = 768
+BIG = 1.0e25
+HOLD = float(2 ** 22)
+DROP = -float(2 ** 24)
+MV = 24
+TW = [512, 448, 384, 384, 256, 256, 128, 128]
+TO = [sum(TW[:t]) for t in range(8)]
+TN = sum(TW)
+STAGE = ((256, 512, 4, 3), (128, 256, 3, 5), (0, 128, 2, 7))
+VORDER = "c31 D c30 r31 c29 r30 c28 q0 r29 c27 r28 c26 r27 c25 r26 c24 q1 r25 q2 r24 q3 T J X0 P0 q4 A0 q5 U0 X1 W0 P1 q6 A1 q7 U1 P2 X2 W1 A2 U2 W2"
+ZORDER = "s00 s10 s20 s30 b0 k0 b1 b2 b3 b4 b5 k1 f00 v31 f10 f31 f20 f30 s01 s11 s21 f01 f11 f21"
+HORDER = "l0 l1 l2 l3 h0 l4 l5 h1 l6 l7 h2 l8 l9 l10 l11 H3"
+
+BF, F32, I32, U16, U8, X4 = "bfloat16", "float32", "int32", "uint16", "uint8", "float8_e4m3fn_x4"
+
+
+def _sb(n, d):
+    return ("sbuf", [128, n], d)
+
+
+SCRATCH = {
+    "xa": _sb(4 * C, BF), "ub": _sb(512, BF), "vb": _sb(512, BF),
+    "uq": _sb(128, X4), "us": _sb(128, U8), "urq": _sb(128, X4), "urs": _sb(128, U8),
+    "vq": _sb(128, X4), "vs": _sb(128, U8), "wq": _sb(512, X4), "wsp": _sb(512, U8),
+    "xq": _sb(512, X4), "xs": _sb(512, U8), "cli": _sb(112, I32), "clu": _sb(112, U16),
+    "ct": _sb(4 * TN, BF), "cq": _sb(TN, X4), "cs": _sb(TN, U8),
+    "one": _sb(512, BF), "half": _sb(512, BF), "quar": _sb(512, BF), "bd1": _sb(512, BF), "bd": _sb(512, BF), "bdq": _sb(128, X4), "bds": _sb(128, U8),
+    "eb": _sb(2048, BF), "ebq": _sb(512, X4), "ebs": _sb(512, U8), "ec": _sb(2048, BF), "ecq": _sb(512, X4), "ecs": _sb(512, U8),
+    "pi": _sb(8, I32), "pf": _sb(16, F32), "r16": _sb(64, BF), "r4": _sb(64, BF), "e64": _sb(256, BF),
+    "i16": _sb(32, F32), "uoi": _sb(8, I32), "uou": _sb(8, U16), "i704": _sb(PL, F32), "io4": _sb(512, F32),
+    "m1": _sb(512, BF), "k1": _sb(512, BF), "rst": _sb(512, BF), "a16": _sb(512, BF), "a4": _sb(192, BF),
+    "base": _sb(32, F32), "own": _sb(32, F32), "ownm": _sb(32, F32), "nb": _sb(12, F32),
+    "mn": _sb(512, F32), "fs": _sb(512, F32), "sg": _sb(8 * MV * (MV - 1), BF), "jr": _sb(256 * (32 - MV), BF),
+    "rs": _sb(32, F32), "dg": _sb(512, BF), "t1": _sb(32, F32), "rp": _sb(32, F32), "cx": _sb(512, F32),
+    "rk": _sb(32, F32), "rku": _sb(32, U16), "ls": _sb(512, F32), "lx": _sb(192, F32), "eo": _sb(48, U16),
+    "et": _sb(4 * K, BF), "eh": _sb(4 * K, BF),
+    "eq": _sb(R * K, X4), "es": _sb(R * K, U8), "gq": _sb(R * K, X4), "gs": _sb(R * K, U8),
+    "rq": _sb(R * K, X4), "rsc": _sb(R * K, U8), "bq": _sb(R * K, X4), "bs": _sb(R * K, U8),
+    "ft": _sb(PL, BF), "ph": _sb(4 * PL, BF), "lr": _sb(4 * A, F32), "lxs": _sb(4 * A, F32),
+    "lc": _sb(112, F32), "ou": _sb(112, U16), "pt": _sb(112, F32), "pay": _sb(112, F32),
+    "lv": _sb(112, I32), "lt": _sb(112, I32), "lw": _sb(28, I32), "wf": _sb(112, F32), "wp": _sb(112, F32),
+    "gf": _sb(4 * A, BF), "fx": _sb(4 * A, BF), "val": _sb(112, F32), "mx1": _sb(56, F32), "mx2": _sb(28, I32),
+    "oti": _sb(56, I32), "otu": _sb(56, U16),
+    "tk": _sb(PL, F32), "enc": _sb(A, F32), "key": _sb(A, F32), "g2": _sb(4 * A, BF), "zt": _sb(4 * A, BF),
+    "zq": _sb(A, X4), "zs": _sb(A, U8), "ab": _sb(12 * A, BF), "jf": _sb(12 * 224, BF), "fo": _sb(12, U16),
+    "ht": _sb(4 * HW, BF), "vt": _sb(4 * K, BF),
+    "u1": _sb(32, F32), "u2": _sb(32, F32), "u3": _sb(32, F32), "uo": _sb(32, U16), "u4": _sb(32, F32),
+    "ci": _sb(28, I32), "cj": _sb(28, I32), "cw": _sb(32, F32), "cwt": _sb(32, F32), "yo": _sb(512, F32),
+    "ps": ("psum", [128, 4096], F32),
+}
+SEMAPHORES = ["cv", "cs_", "ct_", "cg", "ldx0", "ldx1", "ldu", "ldc", "ldw", "lds", "ldv", "sent", "st", "stw"] + \
+    ["ae%d" % r for r in range(R)] + ["ab%d" % r for r in range(R)]
+
+
+def rank_program(g, core, T, topo):
+    rank = T.rank_of(core)
+    if rank is None:
+        return
+    n_ranks = len(T.cores)
+    after, before = T.cores[(rank + 1) % n_ranks], T.cores[(rank - 1) % n_ranks]
+    V, S, PE, SY = g.vector, g.scalar, g.tensor, g.sync
+    queue = {"v": V, "s": S, "t": PE, "g": g, "y": SY}
+    counter = {"v": T.sem["cv"], "s": T.sem["cs_"], "t": T.sem["ct_"], "g": T.sem["cg"]}
+    ops = []
+
+    def op(eng, fn, r="", w="", ext=None, dma=None, acc=False, plain=False):
+        ops.append({"e": eng, "fn": fn, "r": r.split(), "w": w.split(), "ext": ext, "dma": dma, "acc": acc, "plain": plain})
+
+    def ts(out, in0, s1, s2, o0, o1, r, w):
+        if o1 is None:
+            op("v", lambda: V.tensor_scalar(out, in0, s1, None, o0), r, w)
+        else:
+            op("v", lambda: V.tensor_scalar(out, in0, s1, s2, o0, o1), r, w)
+
+    def tt(out, a, b, o, r, w):
+        op("v", lambda: V.tensor_tensor(out, a, b, o), r, w)
+
+    def cp(out, a, r, w):
+        op("v", lambda: V.tensor_copy(out, a), r, w)
+
+    def ms(out, c, w):
+        op("v", lambda: V.memset(out, c), "", w)
+
+    def scan(out, d0, d1, init, o0, o1, r, w):
+        op("v", lambda: V.tensor_tensor_scan(out, d0, d1, init, o0, o1), r, w)
+
+    def qz(q, s, a, r, w):
+        op("v", lambda: V.quantize_mx(q, s, a), r, w)
+
+    def act(out, a, f, r, w, **kw):
+        op("s", lambda: S.activation(out, a, f, **kw), r, w)
+
+    def move(eng, out, a, r, w, by=None):
+        if eng == "s":
+            if by is None:
+                act(out, a, ACT.Copy, r, w)
+            else:
+                act(out, a, ACT.Copy, r, w, scale=by)
+        elif by is None:
+            cp(out, a, r, w)
+        else:
+            ts(out, a, by, None, ALU.mult, None, r, w)
+
+    def mm(bank, n, lq, ls_, rq, rs_, r, start=True, stop=True, ext=None):
+        op("t", lambda: PE.matmul_mx(T.ps[:, 512 * bank:512 * bank + n], lq, ls_, rq, rs_, start, stop), r, "ps%d" % bank,
+           ext=ext, acc=not start)
+
+    def iota(out, pat, base, cm, w, small=True):
+        if small:
+            op("g", lambda: g.iota(out, pat, base, cm, allow_small_or_imprecise_dtypes=True), "", w)
+        else:
+            op("g", lambda: g.iota(out, pat, base, cm), "", w)
+
+    def unit(out, src, b, r, w):
+        op("g", lambda: g.affine_select(out[:, 512 * b:512 * (b + 1)], src[:], [[1, 512]], ALU.is_equal, 0.0, -b, -4), r, w)
+
+    def dma(eng, out, a, sem, r, w):
+        op(eng, lambda: queue[eng].dma_start(out, a), r, w, dma=sem)
+
+    def bank(b, lo, hi):
+        return T.ps[:, 512 * b + lo:512 * b + hi]
+
+    def toks(f, it):
+        return " ".join(f % i for i in it)
+
+    sent = [0]
+
+    def ship(dst, sq, ss, dq, ds, r, sem, tok):
+        rid, pid, _ = topo.addr(dst)
+        m = topo.mask(core, dst)
+        a, b = K * r, K * (r + 1)
+        op("g", lambda: g.remote_dma(dq[:, a:b].bitcast(dt.uint8), sq[:, a:b].bitcast(dt.uint8), sem, T.sem.sent, pid, rid, m), tok, plain=True)
+        op("g", lambda: g.remote_dma(ds[:, a:b], ss[:, a:b], sem, T.sem.sent, pid, rid, m), tok, plain=True)
+        sent[0] += 2 * len(topo.engines(core, dst))
+
+    n_from_before = 2 * len(topo.engines(before, core))
+    n_from_after = 2 * len(topo.engines(after, core))
+
+    def slot(m):
+        t, b = ((32 - m) // 4, (32 - m) % 4) if m else (0, 0)
+        return t, 4 * TO[t] + b
+
+    def slot_view(m, lo, hi):
+        o = slot(m)[1]
+        return T.ct[:, o + 4 * lo:o + 4 * (hi - 1) + 1:4]
+
+    def tile_toks(t):
+        return " ".join("c%d" % m for m in range(32) if slot(m)[0] == t)
+
+    Q, Q1, Q4, Q41, QH, QB, QE, Q512 = (T.pf[:, i:i + 1] for i in (0, 1, 2, 3, 4, 5, 6, 7))
+
+    dma("s", T.ub[:], T.u[:], "ldu", "", "ub")
+    dma("y", T.cli[:], T.cl[:], "ldc", "", "cli")
+    dma("y", T.xa[:, 0:1024], T.x[:, 0:1024], "ldx0", "", toks("x%d", range(4)))
+    dma("s", T.xa[:, 1024:2048], T.x[:, 1024:2048], "ldx1", "", toks("x%d", range(4, 8)))
+
+    iota(T.pi[:, 0:1], [[0, 1]], 0, 1, "pi0", False)
+    iota(T.r16[:], [[0, 4], [1, 16]], 0, 0, "r16")
+    iota(T.uoi[:], [[16, 8]], 0, 0, "uoi", False)
+    iota(T.i16[:], [[16, 32]], 0, 0, "i16")
+    iota(T.r4[:], [[0, 16], [1, 4]], 0, 0, "r4")
+    iota(T.i704[:], [[1, PL]], 0, 0, "i704")
+    ms(T.one[:], 1.0, "one")
+    op("g", lambda: g.affine_select(T.bd1[:], T.one[:], [[16, 8], [0, 64]], ALU.is_ge, 0.0, 15, -1), "one", "bd1")
+    op("g", lambda: g.affine_select(T.bd[:], T.bd1[:], [[-16, 8], [0, 64]], ALU.is_ge, 0.0, 0, 1), "bd1", "bd")
+    iota(T.io4[:], [[4, 512]], 0, 0, "io4")
+    iota(T.lv[:], [[0, 28], [-1, 4]], 3, 0, "lv", False)
+    for t in range(8):
+        lo = 16 * (29 - 4 * t)
+        move("s", T.ct[:, 4 * (TO[t] + lo):4 * (TO[t] + TW[t])], T.one[:, 0:4 * (TW[t] - lo)], "one", tile_toks(t), 0.0)
+    ms(T.k1[:], BIG, "k1")
+    ts(T.pi[:, 1:2], T.pi[:, 0:1], 15, None, ALU.bitwise_and, None, "pi0", "pi1")
+    ms(T.k1[:, 0:512:16], -BIG, "k1")
+    cp(Q, T.pi[:, 1:2], "pi1", "q")
+    cp(T.uou[:], T.uoi[:], "uoi", "uou")
+    ts(T.e64[:, 0:64], T.r16[:], Q, None, ALU.is_equal, None, "r16 q", "e0")
+    ts(Q1, Q, 1.0, None, ALU.add, None, "q", "q1")
+    ts(T.m1[:, 0:64], T.e64[:, 0:64], 2 * BIG, -BIG, ALU.mult, ALU.add, "e0", "m1")
+    ts(T.e64[:, 64:128], T.r16[:], Q1, HOLD, ALU.is_equal, ALU.mult, "r16 q1", "e1")
+    ts(T.e64[:, 128:192], T.e64[:, 0:64], DROP, None, ALU.mult, None, "e0", "e2")
+    cp(T.m1[:, 64:128], T.m1[:, 0:64], "m1", "m1")
+    ts(T.pi[:, 2:3], T.pi[:, 1:2], 2, None, ALU.arith_shift_right, None, "pi1", "pi2")
+    tt(T.a16[:, 0:64], T.e64[:, 64:128], T.e64[:, 128:192], ALU.add, "e1 e2", "a16")
+    cp(T.m1[:, 128:256], T.m1[:, 0:128], "m1", "m1")
+    ts(T.pi[:, 3:4], T.pi[:, 1:2], 3, None, ALU.bitwise_and, None, "pi1", "pi3")
+    cp(T.a16[:, 64:128], T.a16[:, 0:64], "a16", "a16")
+    cp(T.m1[:, 256:512], T.m1[:, 0:256], "m1", "m1")
+    cp(Q4, T.pi[:, 2:3], "pi2", "q4")
+    cp(T.a16[:, 128:256], T.a16[:, 0:128], "a16", "a16")
+    qz(T.uq[:], T.us[:], T.ub[:], "ub", "uq")
+    cp(T.clu[:], T.cli[:], "cli", "clu")
+    cp(T.urq[:].bitcast(dt.uint32), T.uq[:].bitcast(dt.uint32).indirect(T.uou[:]), "uq uou", "urq")
+    cp(T.urs[:], T.us[:].indirect(T.uou[:]), "uq uou", "urs")
+    dma("y", T.wq[:].bitcast(dt.uint8), T.wc[:], "ldw", "urs", "wq")
+    dma("y", T.wsp[:], T.ws[:], "lds", "", "wsp")
+    dma("y", T.vb[:], T.v[:], "ldv", "", "vb")
+
+    def q_half(h):
+        qz(T.xq[:, 256 * h:256 * (h + 1)], T.xs[:, 256 * h:256 * (h + 1)], T.xa[:, 1024 * h:1024 * (h + 1)], toks("x%d", range(4 * h, 4 * h + 4)), "xq%d" % h)
+
+    def clause_rows(h):
+        act(T.lr[:, 896 * h:896 * (h + 1)], T.i704[:].indirect(T.clu[:, 56 * h:56 * (h + 1)]), ACT.Copy, "i704 clu", "lr%d" % h)
+
+    ms(T.rst[:], 1.0, "rst")
+    ts(Q41, Q4, 1.0, None, ALU.add, None, "q4", "q41")
+    ts(QH, Q, 15.0, -HOLD, ALU.is_lt, ALU.mult, "q", "qh")
+    ts(QB, Q, -1.0, 15.0, ALU.mult, ALU.add, "q", "qb")
+    ms(T.rst[:, 0:512:16], 0.0, "rst")
+    q_half(0)
+    cp(T.a16[:, 256:512], T.a16[:, 0:256], "a16", "a16")
+    q_half(1)
+    move("s", T.half[:], T.one[:], "one", "half", 0.5)
+    clause_rows(0)
+    for b in range(4):
+        unit(T.eb, T.half, b, "half", "eb%d" % b)
+    ms(T.rs[:, 0:1], 0.0, "rs0")
+    cp(T.pf[:, 8:9], T.pi[:, 3:4], "pi3", "t4")
+    ts(T.e64[:, 128:192], T.r4[:], Q4, DROP, ALU.is_equal, ALU.mult, "r4 q4", "e2")
+    ts(T.e64[:, 64:128], T.r4[:], Q41, HOLD, ALU.is_equal, ALU.mult, "r4 q41", "e1")
+    ts(T.pf[:, 9:10], Q4, 3.0, -HOLD, ALU.is_lt, ALU.mult, "q4", "qh4")
+    ts(T.base[:], T.i16[:], QB, QH, ALU.add, ALU.add, "i16 qb qh", "base")
+
+    def late_constants():
+        tt(T.a4[:, 0:64], T.e64[:, 64:128], T.e64[:, 128:192], ALU.add, "e1 e2", "a4")
+        tt(QE, T.pf[:, 8:9], T.pf[:, 9:10], ALU.add, "t4 qh4", "qe")
+        move("s", T.a4[:, 64:128], T.a4[:, 0:64], "a4", "a4b")
+        move("s", T.a4[:, 128:192], T.a4[:, 0:64], "a4", "a4c")
+        clause_rows(1)
+        move("s", T.quar[:], T.one[:], "one", "quar", 0.25)
+
+    def clause_tables():
+        for i in range(4):
+            scan(T.lxs[:, A * i:A * (i + 1)], T.a16[:, 0:A], T.lr[:, i:4 * A:4], 0.0, ALU.add, ALU.max, "a16 lr0 lr1", "lxs%d" % i)
+        for i in range(4):
+            ts(T.lc[:, i:112:4], T.lxs[:, A * i + 15:A * (i + 1):16], QH, None, ALU.add, None, "lxs%d qh" % i, "lc%d" % i)
+        ts(T.wf[:], T.lv[:], float(2 ** 20), None, ALU.mult, None, "lv", "wf")
+        cp(T.ou[:], T.lc[:], "lc0 lc1 lc2 lc3", "ou")
+        for i in range(4):
+            ts(T.pt[:, i:112:4], T.lc[:, (i + 1) % 4:112:4], 1024.0, QH, ALU.mult, ALU.add, "lc%d qh" % ((i + 1) % 4), "pt%d" % i)
+
+    def clause_words():
+        tt(T.pay[:], T.pt[:], T.lc[:], ALU.add, "pt0 pt1 pt2 pt3 lc0 lc1 lc2 lc3", "pay")
+        ts(Q512, Q, 512.0, None, ALU.add, None, "q", "q512")
+        tt(T.wp[:], T.wf[:], T.pay[:], ALU.add, "wf pay", "wp")
+        ts(T.nb[:], T.i16[:, 0:12], Q512, -2048.0, ALU.add, ALU.mult, "i16 q512", "nb")
+
+    xall = toks("x%d", range(8))
+    chunks = ((16 * (MV - 8), 16 * MV), (16 * MV, 512), (0, 16 * (MV - 8)))
+
+    for r in range(R):
+        a, b = K * r, K * (r + 1)
+        mm(0, 512, T.urq[:], T.urs[:], T.xq[:], T.xs[:], "urq urs xq0 xq1")
+        mm(1, 512, T.urq[:], T.urs[:], T.xq[:], T.xs[:], "urq urs xq0 xq1")
+
+        def pick_min(h):
+            lo, hi = chunks[h]
+            tt(T.mn[:, lo:hi], bank(0, lo, hi), T.m1[:, lo:hi], ALU.min, "ps0 m1", "mn%d" % h)
+
+        def pick_scan(h):
+            lo, hi = chunks[h]
+            scan(T.fs[:, lo:hi], T.k1[:, lo:hi], T.mn[:, lo:hi], -BIG, ALU.min, ALU.max, "k1 mn%d" % h, "fs%d" % h)
+
+        def fcol(m):
+            return T.fs[:, 16 * m + 15:16 * m + 16], "fs%d" % [h for h in range(3) if chunks[h][0] <= 16 * m < chunks[h][1]][0]
+
+        def s_sign(m):
+            col, tok = fcol(m)
+            o = 8 * m * (m - 1)
+            act(T.sg[:, o:o + 16 * m], bank(1, 0, 16 * m), ACT.Sign, "ps1 " + tok, "sg%d" % m, bias=col, scale=-1.0)
+
+        def s_relu(m):
+            o = 8 * m * (m - 1)
+            act(slot_view(m, 0, 16 * m), T.sg[:, o:o + 16 * m], ACT.Relu, "sg%d" % m, "c%d rs%d" % (m, m), accum_out=T.rs[:, m:m + 1])
+
+        pick_min(0)
+        pick_min(1)
+        pick_scan(0)
+        pick_min(2)
+        pick_scan(1)
+        pick_scan(2)
+        s_sign(MV - 1)
+        for m in range(MV - 1, 0, -1):
+            if m > 1:
+                s_sign(m - 1)
+            s_relu(m)
+
+        def v_cmp(m):
+            col, tok = fcol(m)
+            ts(slot_view(m, 0, 16 * m), bank(0, 0, 16 * m), col, None, ALU.is_lt, None, "ps0 " + tok, "c%d" % m)
+
+        def v_row(m):
+            k = m - MV
+            scan(T.jr[:, 256 * (k + 1) - 8 * m:256 * (k + 1)], slot_view(m, 0, 8 * m), slot_view(m, 8 * m, 16 * m), -248.0, ALU.add, ALU.add,
+                 "c%d" % m, "jr%d" % m)
+
+        def q_tile(t):
+            o = TO[t]
+            qz(T.cq[:, o:o + TW[t]], T.cs[:, o:o + TW[t]], T.ct[:, 4 * o:4 * (o + TW[t])], tile_toks(t), "cq%d" % t)
+            for lo, hi, bk, last in STAGE:
+                if t <= last:
+                    hi = min(hi, TW[t])
+                    mm(bk, hi - lo, T.bdq[:], T.bds[:], T.cq[:, o + lo:o + hi], T.cs[:, o + lo:o + hi], "bdq cq%d" % t, start=t == 0,
+                       stop=t == last_issued[bk])
+
+        def stage(w, k):
+            lo, hi, bk, _ = STAGE[k]
+            m0, m1 = lo // 16, hi // 16
+            if w == "P":
+                tt(T.rp[:, m0:m1], T.t1[:, m0:m1], T.rs[:, m0:m1], ALU.subtract, "t1 " + toks("rs%d", range(m0, m1)), "rp%d" % k)
+            elif w == "X":
+                scan(T.cx[:, lo:hi], T.a16[:, 0:hi - lo], bank(bk, 0, hi - lo), 0.0, ALU.add, ALU.max, "a16 ps%d" % bk, "cx%d" % k)
+            elif w == "A":
+                tt(T.rk[:, m0:m1], T.cx[:, lo + 15:hi:16], T.rp[:, m0:m1], ALU.add, "cx%d rp%d" % (k, k), "rk%d" % k)
+            elif w == "U":
+                cp(T.rku[:, m0:m1], T.rk[:, m0:m1], "rk%d" % k, "rku%d" % k)
+            else:
+                cp(T.ls[:].indirect(T.rku[:, m0:m1]), T.io4[:, lo:hi], "rku%d io4" % k, "ls")
+
+        order = VORDER.split()
+        last_issued = {bk: [int(w[1:]) for w in order if w[0] == "q" and int(w[1:]) <= last][-1] for lo, hi, bk, last in STAGE}
+        tt(slot_view(0, 0, 512), bank(0, 0, 512), T.fs[:], ALU.is_le, "ps0 fs0 fs1 fs2", "c0")
+        for w in order:
+            if w[0] == "c":
+                v_cmp(int(w[1:]))
+            elif w[0] == "r":
+                v_row(int(w[1:]))
+            elif w[0] == "q":
+                if r == 0 and w == "q0":
+                    qz(T.bdq[:], T.bds[:], T.bd[:], "bd", "bdq")
+                q_tile(int(w[1:]))
+            elif w == "D":
+                scan(T.dg[:], T.rst[:], slot_view(0, 0, 512), 0.0, ALU.mult, ALU.add, "rst c0", "dg")
+            elif w == "T":
+                if r == 0:
+                    late_constants()
+                tt(T.t1[:], T.base[:], T.dg[:, 15:512:16], ALU.subtract, "base dg", "t1")
+            elif w == "J":
+                ts(T.rs[:, MV:32], T.jr[:, 255:256 * (32 - MV):256], 248.0, None, ALU.add, None, toks("jr%d", range(MV, 32)), toks("rs%d", range(MV, 32)))
+            else:
+                stage(w[0], int(w[1:]))
+        scan(T.lx[:], T.a4[:], T.ls[:, 0:K], 0.0, ALU.add, ALU.max, "a4 a4b a4c ls", "lx")
+        ts(T.eo[:], T.lx[:, 3:K:4], QE, None, ALU.add, None, "lx qe", "eo")
+        move("s", T.et[:, 384:768], T.xa[:].indirect(T.eo[:, 24:48]), xall + " eo", "et1")
+        move("v", T.et[:, 0:384], T.xa[:].indirect(T.eo[:, 0:24]), xall + " eo", "et0")
+        qz(T.eq[:, a:b], T.es[:, a:b], T.et[:], "et0 et1", "eq%d" % r)
+        ship(after, T.eq, T.es, T.gq, T.gs, r, T.sem["ae%d" % r], "eq%d" % r)
+
+        if r == 0:
+            iota(T.tk[:], [[2048, PL]], 0, 0, "tk")
+            iota(T.enc[:, 0:256], [[1, 256]], 0, 0, "enc0")
+            iota(T.enc[:, 256:384], [[2, 128]], 256, 0, "enc1")
+            iota(T.enc[:, 384:448], [[4, 64]], 512, 0, "enc2")
+            iota(T.ht[:], [[0, 4 * HW]], 0, 0, " ".join("h%d.%d" % (i, j) for i in range(4) for j in range(3)))
+            qz(T.ebq[:], T.ebs[:], T.eb[:], "eb0 eb1 eb2 eb3", "ebq")
+            for t in range(4):
+                unit(T.ec, T.quar, t, "quar", "ec%d" % t)
+        ts(T.ft[:, 0:C], bank(0, 0, 512), 0.0, HOLD, ALU.is_gt, ALU.mult, "ps0", "ft0")
+        for t in range(4):
+            move("s" if t < 2 or r == 0 else "v", T.ph[:, PL * t:PL * t + C], T.xa[:, t:2048:4], xall, "po%d" % t, 0.5)
+        if r == 0:
+            clause_tables()
+        else:
+            move("v", T.eh[:], T.et[:], "et0 et1", "eh", 0.25)
+
+        gq, gs = T.gq[:, a:b], T.gs[:, a:b]
+        mm(2, K, T.urq[:], T.urs[:], gq, gs, "urq urs", ext=(T.sem["ae%d" % r], n_from_before))
+        for t in range(4):
+            mm(4 + t, K, T.ebq[:, 128 * t:128 * (t + 1)], T.ebs[:, 128 * t:128 * (t + 1)], gq, gs, "ebq")
+        ts(T.ft[:, C:PL], bank(2, 0, K), 0.0, HOLD, ALU.is_gt, ALU.mult, "ps2", "ft1")
+        if r == 0:
+            clause_words()
+        part = ((0, 16), (16, 28))
+
+        def flags(eng, k, lo, hi):
+            move(eng, T.gf[:, 16 * lo:16 * hi], T.ft[:].indirect(T.ou[:, lo:hi]), "ft0 ft1 ou", "gf%d" % k)
+
+        def own_flag(k, lo, hi):
+            scan(T.fx[:, 16 * lo:16 * hi], T.a16[:, 0:16 * (hi - lo)], T.gf[:, 16 * lo:16 * hi], 0.0, ALU.add, ALU.max, "a16 gf%d" % k, "fx%d" % k)
+
+        def chain(h):
+            c0, c1 = part[h]
+            n = c1 - c0
+            fx = "fx0 fx1" if h == 0 else "fx2 fx3"
+            return [
+                lambda: tt(T.val[:, 4 * c0:4 * c1], T.fx[:, 64 * c0 + 15:64 * c1:16], T.wp[:, 4 * c0:4 * c1], ALU.add, fx + " wp", "val%d" % h),
+                lambda: tt(T.mx1[:, 2 * c0:2 * c1], T.val[:, 4 * c0:4 * c1:2], T.val[:, 4 * c0 + 1:4 * c1:2], ALU.max, "val%d" % h, "mx1%d" % h),
+                lambda: tt(T.mx2[:, c0:c1], T.mx1[:, 2 * c0:2 * c1:2], T.mx1[:, 2 * c0 + 1:2 * c1:2], ALU.max, "mx1%d" % h, "mx2%d" % h),
+                lambda: ts(T.oti[:, 2 * c0 + n:2 * c1], T.mx2[:, c0:c1], 10, 1023, ALU.arith_shift_right, ALU.bitwise_and, "mx2%d" % h, "otb%d" % h),
+                lambda: ts(T.oti[:, 2 * c0:2 * c0 + n], T.mx2[:, c0:c1], 1023, None, ALU.bitwise_and, None, "mx2%d" % h, "ota%d" % h),
+                lambda: cp(T.otu[:, 2 * c0:2 * c1], T.oti[:, 2 * c0:2 * c1], "ota%d otb%d" % (h, h), "otu%d" % h)]
+
+        def one_of(h):
+            c0, c1 = part[h]
+            return T.otu[:, 2 * c0:c0 + c1]
+
+        def two_of(h):
+            c0, c1 = part[h]
+            return T.otu[:, c0 + c1:2 * c1]
+
+        def second(eng, t, h):
+            lo, hi = 16 * part[h][0], 16 * part[h][1]
+            move(eng, T.g2[:, A * t + lo:A * t + hi], T.ph[:, PL * t:PL * (t + 1)].indirect(two_of(h)), "po%d pi_%d otu%d" % (t, t, h), "g2%d%d" % (t, h))
+
+        def first(t, h):
+            lo, hi = 16 * part[h][0], 16 * part[h][1]
+            tt(T.zt[:, 4 * lo + t:4 * hi:4], T.ph[:, PL * t:PL * (t + 1)].indirect(one_of(h)), T.g2[:, A * t + lo:A * t + hi], ALU.add,
+               "po%d pi_%d otu%d g2%d%d" % (t, t, h, t, h), "zt%d%d" % (t, h))
+
+        def key(h):
+            lo, hi = 16 * part[h][0], 16 * part[h][1]
+            tt(T.key[:, lo:hi], T.tk[:].indirect(one_of(h)), T.enc[:, lo:hi], ALU.add, "tk otu%d enc0 enc1 enc2" % h, "key%d" % h)
+
+        flags("s", 0, 0, 32)
+        flags("v", 1, 32, 64)
+        flags("s", 2, 64, 88)
+        flags("s", 3, 88, 112)
+        own_flag(1, 32, 64)
+        own_flag(0, 0, 32)
+        ca, cb = chain(0), chain(1)
+        ca[0]()
+        ca[1]()
+        own_flag(2, 64, 88)
+        ca[2]()
+        ca[3]()
+        ca[4]()
+        own_flag(3, 88, 112)
+        ca[5]()
+        for t in range(4):
+            move("s", T.ph[:, PL * t + C:PL * (t + 1)], bank(4 + t, 0, K), "ps%d" % (4 + t), "pi_%d" % t)
+        for w in ZORDER.split():
+            if w[0] == "b":
+                cb[int(w[1])]()
+            elif w[0] == "k":
+                key(int(w[1]))
+            elif w[0] == "f":
+                first(int(w[1]), int(w[2]))
+            else:
+                second(w[0], int(w[1]), int(w[2]))
+
+        qz(T.zq[:], T.zs[:], T.zt[:], toks("zt%d0", range(4)) + " " + toks("zt%d1", range(4)), "zq")
+        for t in range(4):
+            mm(4 + t, A, T.wq[:, 128 * t:128 * (t + 1)], T.wsp[:, 128 * t:128 * (t + 1)], T.zq[:], T.zs[:], "wq wsp zq")
+        for m in range(12):
+            act(T.ab[:, A * m:A * (m + 1)], T.key[:], ACT.Abs, "key0 key1 nb", "ab%d" % m, bias=T.nb[:, m:m + 1])
+        for w in HORDER.split():
+            m = int(w[1:])
+            if w[0] == "l":
+                scan(T.jf[:, 224 * m:224 * (m + 1)], T.ab[:, A * m:A * m + 224], T.ab[:, A * m + 224:A * (m + 1)], float(NONE_AT), ALU.min, ALU.min,
+                     "ab%d" % m, "jf%d" % m)
+            else:
+                for j, (lo, hi, at, st) in enumerate(((0, 256, 0, 1), (256, 384, 256, 2), (384, 448, 512, 4))):
+                    o = HW * m + at
+                    move("v" if w[0] == "h" else "s", T.ht[:, o:o + st * (hi - lo):st], bank(4 + m, lo, hi), "ps%d" % (4 + m), "h%d.%d" % (m, j), 0.03125)
+        cp(T.fo[:], T.jf[:, 223:12 * 224:224], toks("jf%d", range(12)), "fo")
+        for t in (0, 1, 2, 3):
+            move("vvss"[t], T.vt[:, t:4 * K:4], T.ht[:, HW * t:HW * (t + 1)].indirect(T.fo[:]), "h%d.0 h%d.1 h%d.2 fo" % (t, t, t), "vt%d" % t)
+        qz(T.rq[:, a:b], T.rsc[:, a:b], T.vt[:], "vt0 vt1 vt2 vt3", "rq%d" % r)
+        ship(before, T.rq, T.rsc, T.bq, T.bs, r, T.sem["ab%d" % r], "rq%d" % r)
+
+        if r == 0:
+            qz(T.ecq[:], T.ecs[:], T.ec[:], "ec0 ec1 ec2 ec3", "ecq")
+            move("s", T.eh[:], T.et[:], "et0 et1", "eh", 0.25)
+            ts(T.own[:], T.i16[:], Q, None, ALU.add, None, "i16 q", "own")
+            ts(T.ownm[:], T.i16[:], Q, -512.0, ALU.add, ALU.add, "i16 q", "ownm")
+        ts(T.u1[:], T.rk[:], float(K), None, ALU.is_lt, None, "rk0 rk1 rk2", "u1")
+        ts(T.lw[:], T.mx2[:], 20, 3, ALU.arith_shift_right, ALU.bitwise_and, "mx20 mx21", "lw")
+        tt(T.u2[:], T.rk[:], T.ownm[:], ALU.subtract, "rk0 rk1 rk2 ownm", "u2")
+        for i in range(4 if r < R - 1 else 1):
+            tt(T.lt[:, i:112:4], T.lv[:, i:112:4], T.lw[:], ALU.subtract, "lv lw", "lt%d" % i)
+        tt(T.u3[:], T.u1[:], T.u2[:], ALU.mult, "u1 u2", "u3")
+        if r < R - 1:
+            ts(T.lt[:], T.lt[:], 3.0, None, ALU.add, None, "lt0 lt1 lt2 lt3", "lt0 lt1 lt2 lt3")
+        else:
+            ts(T.ci[:], T.lt[:, 0:112:4], 4.0, None, ALU.add, None, "lt0", "ci")
+        tt(T.u4[:], T.u3[:], T.own[:], ALU.add, "u3 own", "u4")
+        if r < R - 1:
+            ts(T.lv[:], T.lt[:], 3, None, ALU.bitwise_and, None, "lt0 lt1 lt2 lt3", "lv")
+        else:
+            ts(T.cj[:], T.ci[:], 3, None, ALU.bitwise_and, None, "ci", "cj")
+            ms(T.cw[:, 28:32], 0.0, "cw1")
+        cp(T.uo[:], T.u4[:], "u4", "uo")
+        if r < R - 1:
+            ts(T.wf[:], T.lv[:], float(2 ** 20), None, ALU.mult, None, "lv", "wf")
+            if r == 1:
+                qz(T.vq[:], T.vs[:], T.vb[:], "vb", "vq")
+            tt(T.wp[:], T.wf[:], T.pay[:], ALU.add, "wf pay", "wp")
+        else:
+            cp(T.cw[:, 0:28], T.cj[:], "cj", "cw0")
+            op("v", lambda: V.transpose(T.cwt[:], T.cw[:]), "cw0 cw1", "cwt")
+            for gr in range(8):
+                p0, c0 = 32 * (gr // 2), 16 * (gr % 2)
+                dma("y", T.ow[gr:gr + 1, :], T.cwt[p0:p0 + 28, c0:c0 + 16], "stw", "cwt", "")
+
+        for t in range(4):
+            mm(4 + t, K, T.ecq[:, 128 * t:128 * (t + 1)], T.ecs[:, 128 * t:128 * (t + 1)], T.bq[:, a:b], T.bs[:, a:b], "ecq",
+               ext=(T.sem["ab%d" % r], n_from_after) if t == 0 else None)
+        for t in range(4):
+            tt(T.ph[:, PL * t + C:PL * (t + 1)], bank(4 + t, 0, K), T.eh[:, t:4 * K:4], ALU.add, "ps%d eh" % (4 + t), "pi_%d" % t)
+
+        def renew(eng, t, h):
+            move(eng, T.xa[:, 1024 * h + t:1024 * (h + 1):4], T.ph[:, PL * t:PL * (t + 1)].indirect(T.uo[:, 16 * h:16 * (h + 1)]),
+                 "po%d pi_%d uo" % (t, t), "x%d" % (4 * h + t), 2.0)
+
+        for eng, t, h in (("s", 0, 0), ("s", 1, 0), ("v", 2, 0), ("v", 3, 0), ("s", 0, 1), ("s", 1, 1), ("s", 2, 1)):
+            renew(eng, t, h)
+        q_half(0)
+        renew("v", 3, 1)
+        q_half(1)
+
+    mm(0, 256, T.vq[:], T.vs[:], T.xq[:, 0:256], T.xs[:, 0:256], "vq xq0")
+    mm(1, 256, T.vq[:], T.vs[:], T.xq[:, 256:512], T.xs[:, 256:512], "vq xq1")
+    dma("y", T.oc[:, 0:1024], T.xq[:, 0:256].bitcast(dt.uint8), "st", "xq0", "")
+    move("s", T.yo[:, 0:256], bank(0, 0, 256), "ps0", "yo0")
+    move("v", T.yo[:, 256:512], bank(1, 0, 256), "ps1", "yo1")
+    dma("s", T.y[:, 0:256], T.yo[:, 0:256], "st", "yo0", "")
+    dma("y", T.oc[:, 1024:2048], T.xq[:, 256:512].bitcast(dt.uint8), "st", "xq1", "")
+    for k in range(4):
+        dma("s", T.osc[4 * k:4 * k + 4, :], T.xs[32 * k:32 * k + 4, :], "st", "xq0 xq1", "")
+    dma("y", T.y[:, 256:512], T.yo[:, 256:512], "st", "yo1", "")
+
+    writer, readers, known, seq = {}, {}, {e: {} for e in queue}, {e: 0 for e in queue}
+    for n, o in enumerate(ops):
+        e = o["e"]
+        deps = set()
+        for t in o["r"]:
+            if t in writer:
+                deps.add(writer[t])
+            if t.startswith("ps"):
+                deps.update(d for d in readers.get(t, ()) if ops[d]["e"] != e)
+        for t in o["w"]:
+            if t in writer and not o["acc"]:
+                deps.add(writer[t])
+            deps.update(readers.get(t, ()))
+        for t in o["r"]:
+            readers.setdefault(t, []).append(n)
+        for t in o["w"]:
+            writer[t] = n
+            readers[t] = []
+        deps.discard(n)
+        waits = []
+        for d in sorted(deps, reverse=True):
+            p = ops[d]
+            if known[e].get(p["key"], 0) >= p["seq"]:
+                continue
+            waits.append(d)
+            p["sig"] = True
+            for k2, v2 in p["clock"].items():
+                known[e][k2] = max(known[e].get(k2, 0), v2)
+        o["waits"] = waits
+        if o["dma"]:
+            o["key"], o["seq"] = "dma" + str(n), 1
+        elif o["plain"]:
+            o["key"], o["seq"] = "rem" + str(n), 1
+        else:
+            seq[e] += 1
+            o["key"], o["seq"] = e, seq[e]
+        o["clock"] = dict(known[e])
+        o["clock"][o["key"]] = o["seq"]
+    count = {e: 0 for e in queue}
+    stores = {"st": 0, "stw": 0}
+    for o in ops:
+        e = o["e"]
+        for d in o["waits"]:
+            p = ops[d]
+            if p["dma"]:
+                queue[e].wait_ge(T.sem[p["dma"]], 16)
+            else:
+                queue[e].wait_ge(counter[p["e"]], p["cnt"])
+        if o["ext"]:
+            queue[e].wait_ge(o["ext"][0], o["ext"][1])
+        ins = o["fn"]()
+        if o["dma"]:
+            ins.then_inc(T.sem[o["dma"]], 16)
+            if o["dma"] in stores:
+                stores[o["dma"]] += 16
+        elif o.get("sig"):
+            count[e] += 1
+            o["cnt"] = count[e]
+            ins.then_inc(counter[e], 1)
+    g.wait_ge(T.sem.sent, sent[0])
+    SY.wait_ge(T.sem.stw, stores["stw"])
+    SY.wait_ge(T.sem.st, stores["st"])

@@ -4,22 +4,34 @@ ALU = AluOpType
 ACT = ActivationFunctionType
 
 C, K, A, R = 512, 192, 448, 3
-PL = C + K
-HW = 784
-NONE_AT = 768
+OWN = K + 16
+PL = OWN + C
+HW = 464
+SEG, JG = A + 1, 3
 BIG = 1.0e25
 HOLD = float(2 ** 22)
 DROP = -float(2 ** 24)
-MV = 24
 TW = [512, 448, 384, 384, 256, 256, 128, 128]
+TQ = [512, 448, 384, 320, 256, 192, 128, 128]
 TO = [sum(TW[:t]) for t in range(8)]
 TN = sum(TW)
-STAGE = ((256, 512, 4, 3), (128, 256, 3, 5), (0, 128, 2, 7))
-VORDER = "c31 D c30 r31 c29 r30 c28 q0 r29 c27 r28 c26 r27 c25 r26 c24 q1 r25 q2 r24 q3 T J X0 P0 q4 A0 q5 U0 X1 W0 P1 q6 A1 q7 U1 P2 X2 W1 A2 U2 W2"
-ZORDER = "s00 s10 s20 s30 b0 k0 b1 b2 b3 b4 b5 k1 f00 v31 f10 f31 f20 f30 s01 s11 s21 f01 f11 f21"
-HORDER = "l0 l1 l2 l3 h0 l4 l5 h1 l6 l7 h2 l8 l9 l10 l11 H3"
+STAGE = ((256, 512, 2), (128, 256, 6), (0, 128, 3))
+CHUNK = ((128, 256), (0, 128), (384, 512), (256, 384))
+PART = ((0, 8), (8, 28))
+LISTS = ((0, 8), (16, 36))
+FLAGS = ((0, 16), (16, 32), (32, 64), (64, 96), (96, 112))
+OWNS = ((0, 32), (32, 64), (64, 96), (96, 112))
+MV = 24
+EARLY = (15, 14, 13)
+S_ROWS = EARLY + tuple(m for m in range(MV - 1, 0, -1) if m not in EARLY)
+AHEAD = (13, 9)
+RANK_S = "rn00 rn10 rn01 rn11 rn21"
+RANK_V = ("ad0 ad1 ad2 ad3 rn20 rn30 rn31 qx0 qx1 mn0 mn1 fs0 fs1 mn2 mn3 d0 fs2 fs3 c31 d1 c30 c29 c28 c27 dg c26 c25 q0 c24 r31 r30 r29 q1 r28 r27 q2 "
+          "r26 t1 r25 r24 q3 aw av0 q4 cx0 q5 av1 ru0 cx1 sc0 ru1 q6 av2 q7 sc1 cx2 ru2 sc2 lx eo et0 qe")
+LAYER_V = ("ft1 fl1 fl4 of0 pi0 a1 of3 a2 of1 a3 a4 pi1 a5 of2 en0 b1 z00 b2 z10 b3 b4 z20 b5 z30 en1 en2 qz0 n0 n1 n2 z01 n3 z11 n4 z21 n5 z31 j0 qz1 j1 j2 j3 fo vt0 vt1 qv")
+LAYER_S = "fl0 fl2 fl3 pi2 pi3 s00 s10 s20 s30 k0 k1 s01 s11 s21 s31 n6 n7 n8 n9 n10 n11 h00 h10 h20 h30 h01 h11 h21 h31 vt2 vt3"
 
-BF, F32, I32, U16, U8, X4 = "bfloat16", "float32", "int32", "uint16", "uint8", "float8_e4m3fn_x4"
+BF, F32, I32, U16, U8, X4, F16 = "bfloat16", "float32", "int32", "uint16", "uint8", "float8_e4m3fn_x4", "float16"
 
 
 def _sb(n, d):
@@ -32,25 +44,26 @@ SCRATCH = {
     "vq": _sb(128, X4), "vs": _sb(128, U8), "wq": _sb(512, X4), "wsp": _sb(512, U8),
     "xq": _sb(512, X4), "xs": _sb(512, U8), "cli": _sb(112, I32), "clu": _sb(112, U16),
     "ct": _sb(4 * TN, BF), "cq": _sb(TN, X4), "cs": _sb(TN, U8),
-    "one": _sb(512, BF), "half": _sb(512, BF), "quar": _sb(512, BF), "bd1": _sb(512, BF), "bd": _sb(512, BF), "bdq": _sb(128, X4), "bds": _sb(128, U8),
-    "eb": _sb(2048, BF), "ebq": _sb(512, X4), "ebs": _sb(512, U8), "ec": _sb(2048, BF), "ecq": _sb(512, X4), "ecs": _sb(512, U8),
-    "pi": _sb(8, I32), "pf": _sb(16, F32), "r16": _sb(64, BF), "r4": _sb(64, BF), "e64": _sb(256, BF),
-    "i16": _sb(32, F32), "uoi": _sb(8, I32), "uou": _sb(8, U16), "i704": _sb(PL, F32), "io4": _sb(512, F32),
-    "m1": _sb(512, BF), "k1": _sb(512, BF), "rst": _sb(512, BF), "a16": _sb(512, BF), "a4": _sb(192, BF),
-    "base": _sb(32, F32), "own": _sb(32, F32), "ownm": _sb(32, F32), "nb": _sb(12, F32),
+    "one": _sb(512, BF), "quar": _sb(512, BF), "bd1": _sb(512, BF), "bd": _sb(512, BF), "bdq": _sb(128, X4), "bds": _sb(128, U8),
+    "eb": _sb(2048, BF), "ebq": _sb(512, X4), "ebs": _sb(512, U8),
+    "pi": _sb(8, I32), "pf": _sb(16, F32), "r16": _sb(128, BF), "r16k": _sb(128, F32), "r4": _sb(64, BF), "e0": _sb(128, BF), "e64": _sb(384, BF),
+    "i16": _sb(32, F32), "uoi": _sb(8, I32), "uou": _sb(8, U16), "i704": _sb(C + K, F32), "io4": _sb(512, BF),
+    "m1": _sb(128, BF), "k1": _sb(128, BF), "rst": _sb(512, BF), "a16": _sb(512, BF), "a4": _sb(192, BF), "av": _sb(512, F32),
+    "base": _sb(32, F32), "own": _sb(32, F32), "ownm": _sb(32, F32),
     "mn": _sb(512, F32), "fs": _sb(512, F32), "sg": _sb(8 * MV * (MV - 1), BF), "jr": _sb(256 * (32 - MV), BF),
-    "rs": _sb(32, F32), "dg": _sb(512, BF), "t1": _sb(32, F32), "rp": _sb(32, F32), "cx": _sb(512, F32),
-    "rk": _sb(32, F32), "rku": _sb(32, U16), "ls": _sb(512, F32), "lx": _sb(192, F32), "eo": _sb(48, U16),
+    "rs": _sb(32, F32), "dg": _sb(512, BF), "t1": _sb(32, F32), "cx": _sb(512, F32),
+    "rku": _sb(32, U16), "ls": _sb(512, BF), "lx": _sb(192, F16), "eo": _sb(48, U16),
     "et": _sb(4 * K, BF), "eh": _sb(4 * K, BF),
     "eq": _sb(R * K, X4), "es": _sb(R * K, U8), "gq": _sb(R * K, X4), "gs": _sb(R * K, U8),
     "rq": _sb(R * K, X4), "rsc": _sb(R * K, U8), "bq": _sb(R * K, X4), "bs": _sb(R * K, U8),
     "ft": _sb(PL, BF), "ph": _sb(4 * PL, BF), "lr": _sb(4 * A, F32), "lxs": _sb(4 * A, F32),
     "lc": _sb(112, F32), "ou": _sb(112, U16), "pt": _sb(112, F32), "pay": _sb(112, F32),
     "lv": _sb(112, I32), "lt": _sb(112, I32), "lw": _sb(28, I32), "wf": _sb(112, F32), "wp": _sb(112, F32),
-    "gf": _sb(4 * A, BF), "fx": _sb(4 * A, BF), "val": _sb(112, F32), "mx1": _sb(56, F32), "mx2": _sb(28, I32),
+    "gf": _sb(4 * A, BF), "fx": _sb(4 * A, BF), "val": _sb(112, F32), "dw": _sb(112, F32), "mx2": _sb(28, I32),
     "oti": _sb(56, I32), "otu": _sb(56, U16),
-    "tk": _sb(PL, F32), "enc": _sb(A, F32), "key": _sb(A, F32), "g2": _sb(4 * A, BF), "zt": _sb(4 * A, BF),
-    "zq": _sb(A, X4), "zs": _sb(A, U8), "ab": _sb(12 * A, BF), "jf": _sb(12 * 224, BF), "fo": _sb(12, U16),
+    "pr": _sb(PL, BF), "en0": _sb(SEG, F32), "en": _sb(JG * SEG, F16), "nn": _sb(12 * SEG, BF), "jf": _sb(12 * SEG, F16),
+    "nb": _sb(12, BF), "nbs": _sb(12, F32), "key": _sb(A, BF), "g2": _sb(4 * A, BF), "zt": _sb(4 * A, BF),
+    "zq": _sb(A, X4), "zs": _sb(A, U8), "fo": _sb(12, U16),
     "ht": _sb(4 * HW, BF), "vt": _sb(4 * K, BF),
     "u1": _sb(32, F32), "u2": _sb(32, F32), "u3": _sb(32, F32), "uo": _sb(32, U16), "u4": _sb(32, F32),
     "ci": _sb(28, I32), "cj": _sb(28, I32), "cw": _sb(32, F32), "cwt": _sb(32, F32), "yo": _sb(512, F32),
@@ -69,504 +82,456 @@ def rank_program(g, core, T, topo):
     V, S, PE, SY = g.vector, g.scalar, g.tensor, g.sync
     queue = {"v": V, "s": S, "t": PE, "g": g, "y": SY}
     counter = {"v": T.sem["cv"], "s": T.sem["cs_"], "t": T.sem["ct_"], "g": T.sem["cg"]}
-    ops = []
 
-    def op(eng, fn, r="", w="", ext=None, dma=None, acc=False, plain=False):
-        ops.append({"e": eng, "fn": fn, "r": r.split(), "w": w.split(), "ext": ext, "dma": dma, "acc": acc, "plain": plain})
+    def vw(name, lo=0, hi=None, step=1):
+        return (name, lo, SCRATCH[name][1][1] if hi is None else hi, step)
 
-    def ts(out, in0, s1, s2, o0, o1, r, w):
+    def by(window, offsets):
+        return (window, offsets)
+
+    def ap(x):
+        if not isinstance(x, tuple):
+            return x
+        if len(x) == 2:
+            return ap(x[0]).indirect(ap(x[1]))
+        name, lo, hi, step = x
+        if step < 0:
+            return T[name][:, hi - 1:(lo - 1 if lo else None):step]
+        return T[name][:, lo:hi:step]
+
+    def touched(x):
+        if not isinstance(x, tuple):
+            return []
+        if len(x) == 2:
+            return touched(x[0])
+        name, lo, hi, step = x
+        if name == "ps":
+            return [(name, 1 << (lo // 512))]
+        step = abs(step)
+        n = (hi - lo + step - 1) // step
+        return [(name, (((1 << (step * n)) - 1) // ((1 << step) - 1)) << lo)]
+
+    ops, issue, fresh = [], {e: [] for e in queue}, []
+
+    def op(name, eng, fn, reads, writes, ext=None, dma=None, acc=False, plain=False):
+        r = [t for x in reads for t in touched(x)] + [t for x in list(reads) + list(writes) if isinstance(x, tuple) and len(x) == 2 for t in touched(x[1])]
+        w = [t for x in writes for t in touched(x)]
+        fresh.append(len(ops))
+        ops.append({"name": name, "e": eng, "fn": fn, "r": r, "w": w, "ext": ext, "dma": dma, "acc": acc, "plain": plain})
+
+    def arrange(**orders):
+        for e in queue:
+            mine = [n for n in fresh if ops[n]["e"] == e]
+            if e in orders:
+                place = {w: i for i, w in enumerate(orders[e].split())}
+                mine.sort(key=lambda n: place[ops[n]["name"]])
+            issue[e].extend(mine)
+        del fresh[:]
+
+    def ts(name, out, in0, s1, s2, o0, o1=None):
         if o1 is None:
-            op("v", lambda: V.tensor_scalar(out, in0, s1, None, o0), r, w)
+            op(name, "v", lambda: V.tensor_scalar(ap(out), ap(in0), ap(s1), None, o0), (in0, s1), (out,))
         else:
-            op("v", lambda: V.tensor_scalar(out, in0, s1, s2, o0, o1), r, w)
+            op(name, "v", lambda: V.tensor_scalar(ap(out), ap(in0), ap(s1), ap(s2), o0, o1), (in0, s1, s2), (out,))
 
-    def tt(out, a, b, o, r, w):
-        op("v", lambda: V.tensor_tensor(out, a, b, o), r, w)
+    def tt(name, out, a, b, o):
+        op(name, "v", lambda: V.tensor_tensor(ap(out), ap(a), ap(b), o), (a, b), (out,))
 
-    def cp(out, a, r, w):
-        op("v", lambda: V.tensor_copy(out, a), r, w)
+    def cp(name, out, a):
+        op(name, "v", lambda: V.tensor_copy(ap(out), ap(a)), (a,), (out,))
 
-    def ms(out, c, w):
-        op("v", lambda: V.memset(out, c), "", w)
+    def ms(name, out, c):
+        op(name, "v", lambda: V.memset(ap(out), c), (), (out,))
 
-    def scan(out, d0, d1, init, o0, o1, r, w):
-        op("v", lambda: V.tensor_tensor_scan(out, d0, d1, init, o0, o1), r, w)
+    def scan(name, out, d0, d1, init, o0, o1):
+        op(name, "v", lambda: V.tensor_tensor_scan(ap(out), ap(d0), ap(d1), init, o0, o1), (d0, d1), (out,))
 
-    def qz(q, s, a, r, w):
-        op("v", lambda: V.quantize_mx(q, s, a), r, w)
+    def qz(name, q, s, a):
+        op(name, "v", lambda: V.quantize_mx(ap(q), ap(s), ap(a)), (a,), (q, s))
 
-    def act(out, a, f, r, w, **kw):
-        op("s", lambda: S.activation(out, a, f, **kw), r, w)
+    def act(name, out, a, f, bias=None, scale=None, accum=None):
+        kw = {}
+        for k, x in (("bias", bias), ("scale", scale), ("accum_out", accum)):
+            if x is not None:
+                kw[k] = ap(x)
+        op(name, "s", lambda: S.activation(ap(out), ap(a), f, **kw), (a, bias, scale), (out, accum))
 
-    def move(eng, out, a, r, w, by=None):
+    def move(name, eng, out, a, times=None):
         if eng == "s":
-            if by is None:
-                act(out, a, ACT.Copy, r, w)
-            else:
-                act(out, a, ACT.Copy, r, w, scale=by)
-        elif by is None:
-            cp(out, a, r, w)
+            act(name, out, a, ACT.Copy, scale=times)
+        elif times is None:
+            cp(name, out, a)
         else:
-            ts(out, a, by, None, ALU.mult, None, r, w)
+            ts(name, out, a, times, None, ALU.mult)
 
-    def mm(bank, n, lq, ls_, rq, rs_, r, start=True, stop=True, ext=None):
-        op("t", lambda: PE.matmul_mx(T.ps[:, 512 * bank:512 * bank + n], lq, ls_, rq, rs_, start, stop), r, "ps%d" % bank,
-           ext=ext, acc=not start)
-
-    def iota(out, pat, base, cm, w, small=True):
-        if small:
-            op("g", lambda: g.iota(out, pat, base, cm, allow_small_or_imprecise_dtypes=True), "", w)
-        else:
-            op("g", lambda: g.iota(out, pat, base, cm), "", w)
-
-    def unit(out, src, b, r, w):
-        op("g", lambda: g.affine_select(out[:, 512 * b:512 * (b + 1)], src[:], [[1, 512]], ALU.is_equal, 0.0, -b, -4), r, w)
-
-    def dma(eng, out, a, sem, r, w):
-        op(eng, lambda: queue[eng].dma_start(out, a), r, w, dma=sem)
+    def on(name, s_order):
+        return "s" if name in s_order.split() else "v"
 
     def bank(b, lo, hi):
-        return T.ps[:, 512 * b + lo:512 * b + hi]
+        return vw("ps", 512 * b + lo, 512 * b + hi)
 
-    def toks(f, it):
-        return " ".join(f % i for i in it)
+    def mm(name, b, lq, ls_, at, rq, rs_, lo, hi, start=True, stop=True, ext=None):
+        views = (vw(lq, at, at + 128), vw(ls_, at, at + 128), vw(rq, lo, hi), vw(rs_, lo, hi))
+        op(name, "t", lambda: PE.matmul_mx(ap(bank(b, 0, hi - lo)), *[ap(x) for x in views], start, stop), views, (bank(b, 0, hi - lo),),
+           ext=ext, acc=not start)
+
+    def iota(out, pat, base, cm):
+        if SCRATCH[out[0]][2] == I32:
+            op("", "g", lambda: g.iota(ap(out), pat, base, cm), (), (out,))
+        else:
+            op("", "g", lambda: g.iota(ap(out), pat, base, cm, allow_small_or_imprecise_dtypes=True), (), (out,))
+
+    def select(out, src, pat, cmp, base, cm):
+        op("", "g", lambda: g.affine_select(ap(out), ap(src), pat, cmp, 0.0, base, cm), (src,), (out,))
+
+    def unit(out, src, b):
+        select(vw(out, 512 * b, 512 * (b + 1)), vw(src), [[1, 512]], ALU.is_equal, -b, -4)
+
+    def dma(eng, out, a, sem, reads=(), writes=()):
+        op("", eng, lambda: queue[eng].dma_start(out, a), reads, writes, dma=sem)
 
     sent = [0]
 
-    def ship(dst, sq, ss, dq, ds, r, sem, tok):
+    def ship(dst, sq, ss, dq, ds, r, sem):
         rid, pid, _ = topo.addr(dst)
         m = topo.mask(core, dst)
         a, b = K * r, K * (r + 1)
-        op("g", lambda: g.remote_dma(dq[:, a:b].bitcast(dt.uint8), sq[:, a:b].bitcast(dt.uint8), sem, T.sem.sent, pid, rid, m), tok, plain=True)
-        op("g", lambda: g.remote_dma(ds[:, a:b], ss[:, a:b], sem, T.sem.sent, pid, rid, m), tok, plain=True)
+        op("", "g", lambda: g.remote_dma(T[dq][:, a:b].bitcast(dt.uint8), T[sq][:, a:b].bitcast(dt.uint8), sem, T.sem.sent, pid, rid, m),
+           (vw(sq, a, b),), (), plain=True)
+        op("", "g", lambda: g.remote_dma(T[ds][:, a:b], T[ss][:, a:b], sem, T.sem.sent, pid, rid, m), (vw(ss, a, b),), (), plain=True)
         sent[0] += 2 * len(topo.engines(core, dst))
 
     n_from_before = 2 * len(topo.engines(before, core))
     n_from_after = 2 * len(topo.engines(after, core))
 
-    def slot(m):
-        t, b = ((32 - m) // 4, (32 - m) % 4) if m else (0, 0)
-        return t, 4 * TO[t] + b
-
     def slot_view(m, lo, hi):
-        o = slot(m)[1]
-        return T.ct[:, o + 4 * lo:o + 4 * (hi - 1) + 1:4]
+        t, b = ((32 - m) // 4, (32 - m) % 4) if m else (0, 0)
+        o = 4 * TO[t] + b
+        return vw("ct", o + 4 * lo, o + 4 * (hi - 1) + 1, 4)
 
-    def tile_toks(t):
-        return " ".join("c%d" % m for m in range(32) if slot(m)[0] == t)
-
-    Q, Q1, Q4, Q41, QH, QB, QE, Q512 = (T.pf[:, i:i + 1] for i in (0, 1, 2, 3, 4, 5, 6, 7))
-
-    dma("s", T.ub[:], T.u[:], "ldu", "", "ub")
-    dma("y", T.cli[:], T.cl[:], "ldc", "", "cli")
-    dma("y", T.xa[:, 0:1024], T.x[:, 0:1024], "ldx0", "", toks("x%d", range(4)))
-    dma("s", T.xa[:, 1024:2048], T.x[:, 1024:2048], "ldx1", "", toks("x%d", range(4, 8)))
-
-    iota(T.pi[:, 0:1], [[0, 1]], 0, 1, "pi0", False)
-    iota(T.r16[:], [[0, 4], [1, 16]], 0, 0, "r16")
-    iota(T.uoi[:], [[16, 8]], 0, 0, "uoi", False)
-    iota(T.i16[:], [[16, 32]], 0, 0, "i16")
-    iota(T.r4[:], [[0, 16], [1, 4]], 0, 0, "r4")
-    iota(T.i704[:], [[1, PL]], 0, 0, "i704")
-    ms(T.one[:], 1.0, "one")
-    op("g", lambda: g.affine_select(T.bd1[:], T.one[:], [[16, 8], [0, 64]], ALU.is_ge, 0.0, 15, -1), "one", "bd1")
-    op("g", lambda: g.affine_select(T.bd[:], T.bd1[:], [[-16, 8], [0, 64]], ALU.is_ge, 0.0, 0, 1), "bd1", "bd")
-    iota(T.io4[:], [[4, 512]], 0, 0, "io4")
-    iota(T.lv[:], [[0, 28], [-1, 4]], 3, 0, "lv", False)
-    for t in range(8):
-        lo = 16 * (29 - 4 * t)
-        move("s", T.ct[:, 4 * (TO[t] + lo):4 * (TO[t] + TW[t])], T.one[:, 0:4 * (TW[t] - lo)], "one", tile_toks(t), 0.0)
-    ms(T.k1[:], BIG, "k1")
-    ts(T.pi[:, 1:2], T.pi[:, 0:1], 15, None, ALU.bitwise_and, None, "pi0", "pi1")
-    ms(T.k1[:, 0:512:16], -BIG, "k1")
-    cp(Q, T.pi[:, 1:2], "pi1", "q")
-    cp(T.uou[:], T.uoi[:], "uoi", "uou")
-    ts(T.e64[:, 0:64], T.r16[:], Q, None, ALU.is_equal, None, "r16 q", "e0")
-    ts(Q1, Q, 1.0, None, ALU.add, None, "q", "q1")
-    ts(T.m1[:, 0:64], T.e64[:, 0:64], 2 * BIG, -BIG, ALU.mult, ALU.add, "e0", "m1")
-    ts(T.e64[:, 64:128], T.r16[:], Q1, HOLD, ALU.is_equal, ALU.mult, "r16 q1", "e1")
-    ts(T.e64[:, 128:192], T.e64[:, 0:64], DROP, None, ALU.mult, None, "e0", "e2")
-    cp(T.m1[:, 64:128], T.m1[:, 0:64], "m1", "m1")
-    ts(T.pi[:, 2:3], T.pi[:, 1:2], 2, None, ALU.arith_shift_right, None, "pi1", "pi2")
-    tt(T.a16[:, 0:64], T.e64[:, 64:128], T.e64[:, 128:192], ALU.add, "e1 e2", "a16")
-    cp(T.m1[:, 128:256], T.m1[:, 0:128], "m1", "m1")
-    ts(T.pi[:, 3:4], T.pi[:, 1:2], 3, None, ALU.bitwise_and, None, "pi1", "pi3")
-    cp(T.a16[:, 64:128], T.a16[:, 0:64], "a16", "a16")
-    cp(T.m1[:, 256:512], T.m1[:, 0:256], "m1", "m1")
-    cp(Q4, T.pi[:, 2:3], "pi2", "q4")
-    cp(T.a16[:, 128:256], T.a16[:, 0:128], "a16", "a16")
-    qz(T.uq[:], T.us[:], T.ub[:], "ub", "uq")
-    cp(T.clu[:], T.cli[:], "cli", "clu")
-    cp(T.urq[:].bitcast(dt.uint32), T.uq[:].bitcast(dt.uint32).indirect(T.uou[:]), "uq uou", "urq")
-    cp(T.urs[:], T.us[:].indirect(T.uou[:]), "uq uou", "urs")
-    dma("y", T.wq[:].bitcast(dt.uint8), T.wc[:], "ldw", "urs", "wq")
-    dma("y", T.wsp[:], T.ws[:], "lds", "", "wsp")
-    dma("y", T.vb[:], T.v[:], "ldv", "", "vb")
+    Q, Q4, T4, Q1, Q41, QH, QB, QE, QH4, QK = (vw("pf", i, i + 1) for i in range(10))
 
     def q_half(h):
-        qz(T.xq[:, 256 * h:256 * (h + 1)], T.xs[:, 256 * h:256 * (h + 1)], T.xa[:, 1024 * h:1024 * (h + 1)], toks("x%d", range(4 * h, 4 * h + 4)), "xq%d" % h)
+        qz("qx%d" % h, vw("xq", 256 * h, 256 * (h + 1)), vw("xs", 256 * h, 256 * (h + 1)), vw("xa", 1024 * h, 1024 * (h + 1)))
 
-    def clause_rows(h):
-        act(T.lr[:, 896 * h:896 * (h + 1)], T.i704[:].indirect(T.clu[:, 56 * h:56 * (h + 1)]), ACT.Copy, "i704 clu", "lr%d" % h)
+    dma("s", T.ub[:], T.u[:], "ldu", (), (vw("ub"),))
+    dma("y", T.cli[:], T.cl[:], "ldc", (), (vw("cli"),))
+    dma("y", T.xa[:, 0:1024], T.x[:, 0:1024], "ldx0", (), (vw("xa", 0, 1024),))
+    dma("s", T.xa[:, 1024:2048], T.x[:, 1024:2048], "ldx1", (), (vw("xa", 1024, 2048),))
 
-    ms(T.rst[:], 1.0, "rst")
-    ts(Q41, Q4, 1.0, None, ALU.add, None, "q4", "q41")
-    ts(QH, Q, 15.0, -HOLD, ALU.is_lt, ALU.mult, "q", "qh")
-    ts(QB, Q, -1.0, 15.0, ALU.mult, ALU.add, "q", "qb")
-    ms(T.rst[:, 0:512:16], 0.0, "rst")
+    iota(vw("pi", 0, 1), [[0, 1]], 0, 1)
+    iota(vw("r16"), [[0, 8], [1, 16]], 0, 0)
+    iota(vw("uoi"), [[16, 8]], 0, 0)
+    iota(vw("r16k"), [[0, 8], [8192, 16]], 0, 0)
+    iota(vw("r4"), [[0, 16], [1, 4]], 0, 0)
+    iota(vw("i16"), [[16, 32]], 0, 0)
+    iota(vw("i704", 0, C), [[1, C]], OWN, 0)
+    iota(vw("i704", C, C + K), [[1, K]], 0, 0)
+    ms("", vw("one"), 1.0)
+    select(vw("rst"), vw("one"), [[0, 32], [1, 16]], ALU.is_gt, 0, 0)
+    select(vw("bd1"), vw("one"), [[16, 8], [0, 64]], ALU.is_ge, 15, -1)
+    select(vw("bd"), vw("bd1"), [[-16, 8], [0, 64]], ALU.is_ge, 0, 1)
+    iota(vw("io4"), [[1, 512]], -256, 0)
+    iota(vw("lv"), [[0, 28], [-1, 4]], 3, 0)
+    for t in range(8):
+        lo = 16 * (29 - 4 * t)
+        move("", "s", vw("ct", 4 * (TO[t] + lo), 4 * (TO[t] + TW[t])), vw("one", 0, 4 * (TW[t] - lo)), 0.0)
+    ts("", vw("pi", 1, 2), vw("pi", 0, 1), 15, None, ALU.bitwise_and)
+    ts("", vw("pi", 2, 3), vw("pi", 0, 1), 2, 3, ALU.arith_shift_right, ALU.bitwise_and)
+    ts("", vw("pi", 3, 4), vw("pi", 0, 1), 3, None, ALU.bitwise_and)
+    ts("", vw("k1"), vw("r16"), 0.5, 2 * BIG, ALU.subtract, ALU.mult)
+    cp("", vw("pf", 0, 3), vw("pi", 1, 4))
+    cp("", vw("uou"), vw("uoi"))
+    ts("", vw("e0"), vw("r16"), Q, None, ALU.is_equal)
+    ts("", QK, Q, 8192.0, -4096.0, ALU.mult, ALU.add)
+    ts("", QB, Q, 4095.0, 15.0 - 15 * 4096.0 - 1024.0, ALU.mult, ALU.add)
+    ts("", vw("m1"), vw("e0"), 2 * BIG, -BIG, ALU.mult, ALU.add)
+    ts("", Q41, Q4, 1.0, None, ALU.add)
+    ts("", Q1, Q, 1.0, None, ALU.add)
+    ts("", QH4, Q4, 3.0, -4096.0, ALU.is_lt, ALU.mult)
+    ts("", QH, Q, 15.0, -HOLD, ALU.is_lt, ALU.mult)
+    ts("", vw("av", 0, 128), vw("r16k"), QK, 4096.0, ALU.subtract, ALU.min)
+    ms("", vw("rs", 0, 1), 0.0)
+    ts("", vw("e64", 0, 64), vw("r4"), Q4, -4096.0, ALU.is_equal, ALU.mult)
+    ts("", vw("e64", 64, 128), vw("r4"), Q41, 1024.0, ALU.is_equal, ALU.mult)
+    ts("", vw("e64", 128, 256), vw("e0"), DROP, None, ALU.mult)
+    ts("", vw("e64", 256, 384), vw("r16"), Q1, HOLD, ALU.is_equal, ALU.mult)
+    ts("", vw("base", 0, MV), vw("i16", 0, MV), QB, None, ALU.add)
+    ts("", vw("base", MV, 32), vw("i16", MV, 32), QB, -248.0, ALU.add, ALU.add)
+    tt("", vw("a4", 0, 64), vw("e64", 0, 64), vw("e64", 64, 128), ALU.add)
+    ts("", QE, T4, QH4, 1024.0, ALU.add, ALU.add)
+    tt("", vw("a16", 0, 128), vw("e64", 128, 256), vw("e64", 256, 384), ALU.add)
+    for name, n, end in (("av", 128, 512), ("a4", 64, K), ("a16", 128, 512)):
+        for at in range(n, end, n):
+            move("", "s", vw(name, at, at + n), vw(name, 0, n))
+    op("", "g", lambda: g.affine_select(T.quar[:], T.one[:], [[0, 512]], ALU.is_gt, 0.25, 0, 0), (vw("one"),), (vw("quar"),))
+    cp("", vw("clu"), vw("cli"))
+    qz("", vw("uq"), vw("us"), vw("ub"))
+    op("", "v", lambda: V.tensor_copy(T.urq[:].bitcast(dt.uint32), T.uq[:].bitcast(dt.uint32).indirect(T.uou[:])), (vw("uq"), vw("uou")), (vw("urq"),))
+    cp("", vw("urs"), by(vw("us"), vw("uou")))
+    dma("y", T.wq[:].bitcast(dt.uint8), T.wc[:], "ldw", (vw("urs"),), (vw("wq"),))
+    dma("y", T.wsp[:], T.ws[:], "lds", (), (vw("wsp"),))
+    dma("y", T.vb[:], T.v[:], "ldv", (), (vw("vb"),))
     q_half(0)
-    cp(T.a16[:, 256:512], T.a16[:, 0:256], "a16", "a16")
-    q_half(1)
-    move("s", T.half[:], T.one[:], "one", "half", 0.5)
-    clause_rows(0)
-    for b in range(4):
-        unit(T.eb, T.half, b, "half", "eb%d" % b)
-    ms(T.rs[:, 0:1], 0.0, "rs0")
-    cp(T.pf[:, 8:9], T.pi[:, 3:4], "pi3", "t4")
-    ts(T.e64[:, 128:192], T.r4[:], Q4, DROP, ALU.is_equal, ALU.mult, "r4 q4", "e2")
-    ts(T.e64[:, 64:128], T.r4[:], Q41, HOLD, ALU.is_equal, ALU.mult, "r4 q41", "e1")
-    ts(T.pf[:, 9:10], Q4, 3.0, -HOLD, ALU.is_lt, ALU.mult, "q4", "qh4")
-    ts(T.base[:], T.i16[:], QB, QH, ALU.add, ALU.add, "i16 qb qh", "base")
 
-    def late_constants():
-        tt(T.a4[:, 0:64], T.e64[:, 64:128], T.e64[:, 128:192], ALU.add, "e1 e2", "a4")
-        tt(QE, T.pf[:, 8:9], T.pf[:, 9:10], ALU.add, "t4 qh4", "qe")
-        move("s", T.a4[:, 64:128], T.a4[:, 0:64], "a4", "a4b")
-        move("s", T.a4[:, 128:192], T.a4[:, 0:64], "a4", "a4c")
-        clause_rows(1)
-        move("s", T.quar[:], T.one[:], "one", "quar", 0.25)
+    def clause_rows(name, lo, hi):
+        move(name, "s", vw("lr", 16 * lo, 16 * hi), by(vw("i704"), vw("clu", lo, hi)))
+
+    clause_rows("", 0, 40)
+    for b in range(4):
+        unit("eb", "quar", b)
+    iota(vw("en0"), [[1, SEG]], 0, 0)
+    iota(vw("ft", K, OWN), [[0, 16]], 0, 0)
+    for t in range(4):
+        iota(vw("ph", PL * t + K, PL * t + OWN), [[0, 16]], 0, 0)
+    iota(vw("ht", A, 4 * HW, HW), [[0, 4]], 0, 0)
+    arrange()
+
+    def words(between):
+        tt("", vw("wp"), vw("wf"), vw("pay"), ALU.add)
+        between()
+        for i in range(1, 4):
+            tt("", vw("dw", i, 112, 4), vw("wp", i - 1, 112, 4), vw("wp", i, 112, 4), ALU.subtract)
 
     def clause_tables():
         for i in range(4):
-            scan(T.lxs[:, A * i:A * (i + 1)], T.a16[:, 0:A], T.lr[:, i:4 * A:4], 0.0, ALU.add, ALU.max, "a16 lr0 lr1", "lxs%d" % i)
-        for i in range(4):
-            ts(T.lc[:, i:112:4], T.lxs[:, A * i + 15:A * (i + 1):16], QH, None, ALU.add, None, "lxs%d qh" % i, "lc%d" % i)
-        ts(T.wf[:], T.lv[:], float(2 ** 20), None, ALU.mult, None, "lv", "wf")
-        cp(T.ou[:], T.lc[:], "lc0 lc1 lc2 lc3", "ou")
-        for i in range(4):
-            ts(T.pt[:, i:112:4], T.lc[:, (i + 1) % 4:112:4], 1024.0, QH, ALU.mult, ALU.add, "lc%d qh" % ((i + 1) % 4), "pt%d" % i)
-
-    def clause_words():
-        tt(T.pay[:], T.pt[:], T.lc[:], ALU.add, "pt0 pt1 pt2 pt3 lc0 lc1 lc2 lc3", "pay")
-        ts(Q512, Q, 512.0, None, ALU.add, None, "q", "q512")
-        tt(T.wp[:], T.wf[:], T.pay[:], ALU.add, "wf pay", "wp")
-        ts(T.nb[:], T.i16[:, 0:12], Q512, -2048.0, ALU.add, ALU.mult, "i16 q512", "nb")
-
-    xall = toks("x%d", range(8))
-    chunks = ((16 * (MV - 8), 16 * MV), (16 * MV, 512), (0, 16 * (MV - 8)))
+            scan("", vw("lxs", A * i, A * (i + 1)), vw("a16", 0, A), vw("lr", i, 4 * A, 4), 0.0, ALU.add, ALU.max)
+            if i:
+                ts("", vw("lc", i - 1, 112, 4), vw("lxs", A * (i - 1) + 15, A * i, 16), QH, None, ALU.add)
+        ts("", vw("wf"), vw("lv"), float(2 ** 20), None, ALU.mult)
+        ts("", vw("nb"), vw("i16", 0, 12), Q, None, ALU.add)
+        ts("", vw("nbs"), vw("i16", 0, 12), Q, -1024.0, ALU.add, ALU.mult)
+        ts("", vw("lc", 3, 112, 4), vw("lxs", A * 3 + 15, A * 4, 16), QH, None, ALU.add)
+        for i in (3, 0, 1, 2):
+            ts("", vw("pt", i, 112, 4), vw("lc", (i + 1) % 4, 112, 4), 1024.0, QH, ALU.mult, ALU.add)
+        cp("", vw("ou"), vw("lc"))
+        ms("", vw("nn", A, 12 * SEG, SEG), 0.0)
+        ms("", vw("dw", 0, 112, 4), 2 * DROP)
+        tt("", vw("pay"), vw("pt"), vw("lc"), ALU.add)
+        words(lambda: qz("", vw("ebq"), vw("ebs"), vw("eb")))
 
     for r in range(R):
         a, b = K * r, K * (r + 1)
-        mm(0, 512, T.urq[:], T.urs[:], T.xq[:], T.xs[:], "urq urs xq0 xq1")
-        mm(1, 512, T.urq[:], T.urs[:], T.xq[:], T.xs[:], "urq urs xq0 xq1")
+        for bk in (4, 5):
+            mm("", bk, "urq", "urs", 0, "xq", "xs", 0, 256)
+        q_half(1)
+        for bk in (0, 1):
+            mm("", bk, "urq", "urs", 0, "xq", "xs", 0, 512)
+        if r == 0:
+            qz("q0", vw("bdq"), vw("bds"), vw("bd"))
 
-        def pick_min(h):
-            lo, hi = chunks[h]
-            tt(T.mn[:, lo:hi], bank(0, lo, hi), T.m1[:, lo:hi], ALU.min, "ps0 m1", "mn%d" % h)
-
-        def pick_scan(h):
-            lo, hi = chunks[h]
-            scan(T.fs[:, lo:hi], T.k1[:, lo:hi], T.mn[:, lo:hi], -BIG, ALU.min, ALU.max, "k1 mn%d" % h, "fs%d" % h)
-
-        def fcol(m):
-            return T.fs[:, 16 * m + 15:16 * m + 16], "fs%d" % [h for h in range(3) if chunks[h][0] <= 16 * m < chunks[h][1]][0]
-
-        def s_sign(m):
-            col, tok = fcol(m)
-            o = 8 * m * (m - 1)
-            act(T.sg[:, o:o + 16 * m], bank(1, 0, 16 * m), ACT.Sign, "ps1 " + tok, "sg%d" % m, bias=col, scale=-1.0)
-
-        def s_relu(m):
-            o = 8 * m * (m - 1)
-            act(slot_view(m, 0, 16 * m), T.sg[:, o:o + 16 * m], ACT.Relu, "sg%d" % m, "c%d rs%d" % (m, m), accum_out=T.rs[:, m:m + 1])
-
-        pick_min(0)
-        pick_min(1)
-        pick_scan(0)
-        pick_min(2)
-        pick_scan(1)
-        pick_scan(2)
-        s_sign(MV - 1)
-        for m in range(MV - 1, 0, -1):
-            if m > 1:
-                s_sign(m - 1)
-            s_relu(m)
-
-        def v_cmp(m):
-            col, tok = fcol(m)
-            ts(slot_view(m, 0, 16 * m), bank(0, 0, 16 * m), col, None, ALU.is_lt, None, "ps0 " + tok, "c%d" % m)
-
-        def v_row(m):
-            k = m - MV
-            scan(T.jr[:, 256 * (k + 1) - 8 * m:256 * (k + 1)], slot_view(m, 0, 8 * m), slot_view(m, 8 * m, 16 * m), -248.0, ALU.add, ALU.add,
-                 "c%d" % m, "jr%d" % m)
-
-        def q_tile(t):
-            o = TO[t]
-            qz(T.cq[:, o:o + TW[t]], T.cs[:, o:o + TW[t]], T.ct[:, 4 * o:4 * (o + TW[t])], tile_toks(t), "cq%d" % t)
-            for lo, hi, bk, last in STAGE:
-                if t <= last:
-                    hi = min(hi, TW[t])
-                    mm(bk, hi - lo, T.bdq[:], T.bds[:], T.cq[:, o + lo:o + hi], T.cs[:, o + lo:o + hi], "bdq cq%d" % t, start=t == 0,
-                       stop=t == last_issued[bk])
-
-        def stage(w, k):
-            lo, hi, bk, _ = STAGE[k]
+        for h, (lo, hi) in enumerate(CHUNK):
+            tt("mn%d" % h, vw("mn", lo, hi), bank(4 if hi <= 256 else 0, lo, hi), vw("m1"), ALU.min)
+            scan("fs%d" % h, vw("fs", lo, hi), vw("k1"), vw("mn", lo, hi), -BIG, ALU.min, ALU.max)
+        for h, (lo, hi) in enumerate(((0, 256), (256, 512))):
+            tt("d%d" % h, slot_view(0, lo, hi), bank(0 if h else 4, lo, hi), vw("fs", lo, hi), ALU.is_le)
+        scan("dg", vw("dg"), vw("rst"), slot_view(0, 0, 512), 0.0, ALU.mult, ALU.add)
+        tt("t1", vw("t1"), vw("base"), vw("dg", 15, 512, 16), ALU.subtract)
+        for m in range(31, 0, -1):
+            col = vw("fs", 16 * m + 15, 16 * m + 16)
+            if m in S_ROWS:
+                sg = vw("sg", 8 * m * (m - 1), 8 * m * (m + 1))
+                act("g%d" % m, sg, bank(5 if m in EARLY else 1, 0, 16 * m), ACT.Sign, bias=col, scale=-1.0)
+                act("p%d" % m, slot_view(m, 0, 16 * m), sg, ACT.Relu, accum=vw("rs", m, m + 1))
+            else:
+                ts("c%d" % m, slot_view(m, 0, 16 * m), bank(4 if m in EARLY else 0, 0, 16 * m), col, None, ALU.is_lt)
+                scan("r%d" % m, vw("jr", 256 * (m - MV + 1) - 8 * m, 256 * (m - MV + 1)), slot_view(m, 0, 8 * m), slot_view(m, 8 * m, 16 * m), -248.0, ALU.add, ALU.add)
+        tiles = [int(w[1:]) for w in RANK_V.split() if w[0] == "q" and w[1:].isdigit()]
+        for t in tiles:
+            o, n = TO[t], (TQ if r else TW)[t]
+            qz("q%d" % t, vw("cq", o, o + n), vw("cs", o, o + n), vw("ct", 4 * o, 4 * (o + n)))
+            for lo, hi, bk in STAGE:
+                adding = [u for u in tiles if TW[u] > lo]
+                if t in adding:
+                    mm("", bk, "bdq", "bds", 0, "cq", "cs", o + lo, o + min(hi, TW[t]), start=t == adding[0], stop=t == adding[-1])
+        tt("aw", vw("av", 16 * MV + 15, 512, 16), vw("t1", MV, 32), vw("jr", 255, 256 * (32 - MV), 256), ALU.subtract)
+        for k, (lo, hi, bk) in enumerate(STAGE):
             m0, m1 = lo // 16, hi // 16
-            if w == "P":
-                tt(T.rp[:, m0:m1], T.t1[:, m0:m1], T.rs[:, m0:m1], ALU.subtract, "t1 " + toks("rs%d", range(m0, m1)), "rp%d" % k)
-            elif w == "X":
-                scan(T.cx[:, lo:hi], T.a16[:, 0:hi - lo], bank(bk, 0, hi - lo), 0.0, ALU.add, ALU.max, "a16 ps%d" % bk, "cx%d" % k)
-            elif w == "A":
-                tt(T.rk[:, m0:m1], T.cx[:, lo + 15:hi:16], T.rp[:, m0:m1], ALU.add, "cx%d rp%d" % (k, k), "rk%d" % k)
-            elif w == "U":
-                cp(T.rku[:, m0:m1], T.rk[:, m0:m1], "rk%d" % k, "rku%d" % k)
-            else:
-                cp(T.ls[:].indirect(T.rku[:, m0:m1]), T.io4[:, lo:hi], "rku%d io4" % k, "ls")
-
-        order = VORDER.split()
-        last_issued = {bk: [int(w[1:]) for w in order if w[0] == "q" and int(w[1:]) <= last][-1] for lo, hi, bk, last in STAGE}
-        tt(slot_view(0, 0, 512), bank(0, 0, 512), T.fs[:], ALU.is_le, "ps0 fs0 fs1 fs2", "c0")
-        for w in order:
-            if w[0] == "c":
-                v_cmp(int(w[1:]))
-            elif w[0] == "r":
-                v_row(int(w[1:]))
-            elif w[0] == "q":
-                if r == 0 and w == "q0":
-                    qz(T.bdq[:], T.bds[:], T.bd[:], "bd", "bdq")
-                q_tile(int(w[1:]))
-            elif w == "D":
-                scan(T.dg[:], T.rst[:], slot_view(0, 0, 512), 0.0, ALU.mult, ALU.add, "rst c0", "dg")
-            elif w == "T":
-                if r == 0:
-                    late_constants()
-                tt(T.t1[:], T.base[:], T.dg[:, 15:512:16], ALU.subtract, "base dg", "t1")
-            elif w == "J":
-                ts(T.rs[:, MV:32], T.jr[:, 255:256 * (32 - MV):256], 248.0, None, ALU.add, None, toks("jr%d", range(MV, 32)), toks("rs%d", range(MV, 32)))
-            else:
-                stage(w[0], int(w[1:]))
-        scan(T.lx[:], T.a4[:], T.ls[:, 0:K], 0.0, ALU.add, ALU.max, "a4 a4b a4c ls", "lx")
-        ts(T.eo[:], T.lx[:, 3:K:4], QE, None, ALU.add, None, "lx qe", "eo")
-        move("s", T.et[:, 384:768], T.xa[:].indirect(T.eo[:, 24:48]), xall + " eo", "et1")
-        move("v", T.et[:, 0:384], T.xa[:].indirect(T.eo[:, 0:24]), xall + " eo", "et0")
-        qz(T.eq[:, a:b], T.es[:, a:b], T.et[:], "et0 et1", "eq%d" % r)
-        ship(after, T.eq, T.es, T.gq, T.gs, r, T.sem["ae%d" % r], "eq%d" % r)
+            tt("av%d" % k, vw("av", lo + 15, 16 * min(m1, MV), 16), vw("t1", m0, min(m1, MV)), vw("rs", m0, min(m1, MV)), ALU.subtract)
+            scan("cx%d" % k, vw("cx", lo, hi), bank(bk, 0, hi - lo), vw("av", lo, hi), -1.0, ALU.max, ALU.add)
+            ts("ru%d" % k, vw("rku", m0, m1), vw("cx", lo + 15, hi, 16), 1024.0, None, ALU.add)
+            cp("sc%d" % k, by(vw("ls"), vw("rku", m0, m1)), vw("io4", lo, hi))
+        if r == 0:
+            clause_rows("late", 40, 112)
+        scan("lx", vw("lx"), vw("a4"), vw("ls", 0, K), 0.0, ALU.add, ALU.max)
+        ts("eo", vw("eo"), vw("lx", 3, K, 4), 4.0, QE, ALU.mult, ALU.add)
+        move("et1", "s", vw("et", 384, 768), by(vw("xa"), vw("eo", 24, 48)))
+        move("et0", "v", vw("et", 0, 384), by(vw("xa"), vw("eo", 0, 24)))
+        qz("qe", vw("eq", a, b), vw("es", a, b), vw("et"))
+        ship(after, "eq", "es", "gq", "gs", r, T.sem["ae%d" % r])
+        rows, todo = [], list(S_ROWS)
+        for i, m in enumerate(S_ROWS):
+            while todo and len(S_ROWS) - len(todo) <= i + (1 if m >= AHEAD[0] else 2 if m >= AHEAD[1] else 4):
+                rows.append("g%d" % todo.pop(0))
+            rows.append("p%d" % m)
+        arrange(v=RANK_V, s=RANK_S + " " + " ".join(rows) + " late et1")
 
         if r == 0:
-            iota(T.tk[:], [[2048, PL]], 0, 0, "tk")
-            iota(T.enc[:, 0:256], [[1, 256]], 0, 0, "enc0")
-            iota(T.enc[:, 256:384], [[2, 128]], 256, 0, "enc1")
-            iota(T.enc[:, 384:448], [[4, 64]], 512, 0, "enc2")
-            iota(T.ht[:], [[0, 4 * HW]], 0, 0, " ".join("h%d.%d" % (i, j) for i in range(4) for j in range(3)))
-            qz(T.ebq[:], T.ebs[:], T.eb[:], "eb0 eb1 eb2 eb3", "ebq")
-            for t in range(4):
-                unit(T.ec, T.quar, t, "quar", "ec%d" % t)
-        ts(T.ft[:, 0:C], bank(0, 0, 512), 0.0, HOLD, ALU.is_gt, ALU.mult, "ps0", "ft0")
+            iota(vw("pr"), [[1, PL]], 0, 0)
+        if r == 0:
+            act("", vw("ft", OWN, PL), bank(1, 0, 512), ACT.Sign)
+        else:
+            words(lambda: ts("", vw("ft", OWN, PL), bank(0, 0, 512), 0.0, None, ALU.is_gt))
         for t in range(4):
-            move("s" if t < 2 or r == 0 else "v", T.ph[:, PL * t:PL * t + C], T.xa[:, t:2048:4], xall, "po%d" % t, 0.5)
+            move("", "s" if t < 3 or r == 0 else "v", vw("ph", PL * t + OWN, PL * (t + 1)), vw("xa", t, 2048, 4), 0.5)
         if r == 0:
             clause_tables()
         else:
-            move("v", T.eh[:], T.et[:], "et0 et1", "eh", 0.25)
+            move("", "v", vw("eh"), vw("et"), 0.25)
+        if r == 1:
+            qz("", vw("vq"), vw("vs"), vw("vb"))
+        arrange()
 
-        gq, gs = T.gq[:, a:b], T.gs[:, a:b]
-        mm(2, K, T.urq[:], T.urs[:], gq, gs, "urq urs", ext=(T.sem["ae%d" % r], n_from_before))
+        mm("", 2, "urq", "urs", 0, "gq", "gs", a, b, ext=(T.sem["ae%d" % r], n_from_before))
         for t in range(4):
-            mm(4 + t, K, T.ebq[:, 128 * t:128 * (t + 1)], T.ebs[:, 128 * t:128 * (t + 1)], gq, gs, "ebq")
-        ts(T.ft[:, C:PL], bank(2, 0, K), 0.0, HOLD, ALU.is_gt, ALU.mult, "ps2", "ft1")
-        if r == 0:
-            clause_words()
-        part = ((0, 16), (16, 28))
-
-        def flags(eng, k, lo, hi):
-            move(eng, T.gf[:, 16 * lo:16 * hi], T.ft[:].indirect(T.ou[:, lo:hi]), "ft0 ft1 ou", "gf%d" % k)
-
-        def own_flag(k, lo, hi):
-            scan(T.fx[:, 16 * lo:16 * hi], T.a16[:, 0:16 * (hi - lo)], T.gf[:, 16 * lo:16 * hi], 0.0, ALU.add, ALU.max, "a16 gf%d" % k, "fx%d" % k)
-
-        def chain(h):
-            c0, c1 = part[h]
-            n = c1 - c0
-            fx = "fx0 fx1" if h == 0 else "fx2 fx3"
-            return [
-                lambda: tt(T.val[:, 4 * c0:4 * c1], T.fx[:, 64 * c0 + 15:64 * c1:16], T.wp[:, 4 * c0:4 * c1], ALU.add, fx + " wp", "val%d" % h),
-                lambda: tt(T.mx1[:, 2 * c0:2 * c1], T.val[:, 4 * c0:4 * c1:2], T.val[:, 4 * c0 + 1:4 * c1:2], ALU.max, "val%d" % h, "mx1%d" % h),
-                lambda: tt(T.mx2[:, c0:c1], T.mx1[:, 2 * c0:2 * c1:2], T.mx1[:, 2 * c0 + 1:2 * c1:2], ALU.max, "mx1%d" % h, "mx2%d" % h),
-                lambda: ts(T.oti[:, 2 * c0 + n:2 * c1], T.mx2[:, c0:c1], 10, 1023, ALU.arith_shift_right, ALU.bitwise_and, "mx2%d" % h, "otb%d" % h),
-                lambda: ts(T.oti[:, 2 * c0:2 * c0 + n], T.mx2[:, c0:c1], 1023, None, ALU.bitwise_and, None, "mx2%d" % h, "ota%d" % h),
-                lambda: cp(T.otu[:, 2 * c0:2 * c1], T.oti[:, 2 * c0:2 * c1], "ota%d otb%d" % (h, h), "otu%d" % h)]
-
-        def one_of(h):
-            c0, c1 = part[h]
-            return T.otu[:, 2 * c0:c0 + c1]
-
-        def two_of(h):
-            c0, c1 = part[h]
-            return T.otu[:, c0 + c1:2 * c1]
-
-        def second(eng, t, h):
-            lo, hi = 16 * part[h][0], 16 * part[h][1]
-            move(eng, T.g2[:, A * t + lo:A * t + hi], T.ph[:, PL * t:PL * (t + 1)].indirect(two_of(h)), "po%d pi_%d otu%d" % (t, t, h), "g2%d%d" % (t, h))
-
-        def first(t, h):
-            lo, hi = 16 * part[h][0], 16 * part[h][1]
-            tt(T.zt[:, 4 * lo + t:4 * hi:4], T.ph[:, PL * t:PL * (t + 1)].indirect(one_of(h)), T.g2[:, A * t + lo:A * t + hi], ALU.add,
-               "po%d pi_%d otu%d g2%d%d" % (t, t, h, t, h), "zt%d%d" % (t, h))
-
-        def key(h):
-            lo, hi = 16 * part[h][0], 16 * part[h][1]
-            tt(T.key[:, lo:hi], T.tk[:].indirect(one_of(h)), T.enc[:, lo:hi], ALU.add, "tk otu%d enc0 enc1 enc2" % h, "key%d" % h)
-
-        flags("s", 0, 0, 32)
-        flags("v", 1, 32, 64)
-        flags("s", 2, 64, 88)
-        flags("s", 3, 88, 112)
-        own_flag(1, 32, 64)
-        own_flag(0, 0, 32)
-        ca, cb = chain(0), chain(1)
-        ca[0]()
-        ca[1]()
-        own_flag(2, 64, 88)
-        ca[2]()
-        ca[3]()
-        ca[4]()
-        own_flag(3, 88, 112)
-        ca[5]()
-        for t in range(4):
-            move("s", T.ph[:, PL * t + C:PL * (t + 1)], bank(4 + t, 0, K), "ps%d" % (4 + t), "pi_%d" % t)
-        for w in ZORDER.split():
-            if w[0] == "b":
-                cb[int(w[1])]()
-            elif w[0] == "k":
-                key(int(w[1]))
-            elif w[0] == "f":
-                first(int(w[1]), int(w[2]))
+            mm("", 4 + t, "ebq", "ebs", 128 * t, "gq", "gs", a, b)
+        ts("ft1", vw("ft", 0, K), bank(2, 0, K), 0.0, None, ALU.is_gt)
+        for k, (lo, hi) in enumerate(FLAGS):
+            named = by(vw("ft"), vw("ou", lo, hi))
+            if on("fl%d" % k, LAYER_S) == "s":
+                act("fl%d" % k, vw("gf", 16 * lo, 16 * hi), named, ACT.Relu, scale=HOLD)
             else:
-                second(w[0], int(w[1]), int(w[2]))
-
-        qz(T.zq[:], T.zs[:], T.zt[:], toks("zt%d0", range(4)) + " " + toks("zt%d1", range(4)), "zq")
+                ts("fl%d" % k, vw("gf", 16 * lo, 16 * hi), named, 0.0, HOLD, ALU.max, ALU.mult)
+        for k, (lo, hi) in enumerate(OWNS):
+            scan("of%d" % k, vw("fx", 16 * lo, 16 * hi), vw("a16", 0, 16 * (hi - lo)), vw("gf", 16 * lo, 16 * hi), 0.0, ALU.add, ALU.max)
+        for h, (c0, c1) in enumerate(PART):
+            w, (o1, o2) = "ab"[h], LISTS[h]
+            scan(w + "1", vw("val", 4 * c0, 4 * c1), vw("dw", 4 * c0, 4 * c1), vw("fx", 64 * c0 + 15, 64 * c1, 16), 0.0, ALU.add, ALU.max)
+            tt(w + "2", vw("mx2", c0, c1), vw("val", 4 * c0 + 3, 4 * c1, 4), vw("wp", 4 * c0 + 3, 4 * c1, 4), ALU.add)
+            ts(w + "3", vw("oti", o2, o2 + c1 - c0), vw("mx2", c0, c1), 10, 1023, ALU.arith_shift_right, ALU.bitwise_and)
+            ts(w + "4", vw("oti", o1, o1 + c1 - c0), vw("mx2", c0, c1), 1023, None, ALU.bitwise_and)
+            cp(w + "5", vw("otu", 2 * c0, 2 * c1), vw("oti", 2 * c0, 2 * c1))
         for t in range(4):
-            mm(4 + t, A, T.wq[:, 128 * t:128 * (t + 1)], T.wsp[:, 128 * t:128 * (t + 1)], T.zq[:], T.zs[:], "wq wsp zq")
+            move("pi%d" % t, on("pi%d" % t, LAYER_S), vw("ph", PL * t, PL * t + K), bank(4 + t, 0, K), 2.0)
+
+        for h, (c0, c1) in enumerate(PART):
+            lo, hi = 16 * c0, 16 * c1
+            one, two = (vw("otu", o, o + c1 - c0) for o in LISTS[h])
+            move("k%d" % h, on("k%d" % h, LAYER_S), vw("key", lo, hi), by(vw("pr"), one))
+            for t in range(4):
+                plane, w = vw("ph", PL * t, PL * (t + 1)), "%d%d" % (t, h)
+                move("s" + w, on("s" + w, LAYER_S), vw("g2", A * t + lo, A * t + hi), by(plane, two))
+                tt("z" + w, vw("zt", 4 * lo + t, 4 * hi, 4), by(plane, one), vw("g2", A * t + lo, A * t + hi), ALU.add)
+            qz("qz%d" % h, vw("zq", lo, hi), vw("zs", lo, hi), vw("zt", 4 * lo, 4 * hi))
+            for t in range(4):
+                bk, w = 4 * (1 - h) + t, "h%d%d" % (t, h)
+                mm("", bk, "wq", "wsp", 128 * t, "zq", "zs", lo, hi)
+                move(w, on(w, LAYER_S), vw("ht", HW * t + lo, HW * t + hi), bank(bk, 0, hi - lo), 0.03125)
         for m in range(12):
-            act(T.ab[:, A * m:A * (m + 1)], T.key[:], ACT.Abs, "key0 key1 nb", "ab%d" % m, bias=T.nb[:, m:m + 1])
-        for w in HORDER.split():
-            m = int(w[1:])
-            if w[0] == "l":
-                scan(T.jf[:, 224 * m:224 * (m + 1)], T.ab[:, A * m:A * m + 224], T.ab[:, A * m + 224:A * (m + 1)], float(NONE_AT), ALU.min, ALU.min,
-                     "ab%d" % m, "jf%d" % m)
+            if on("n%d" % m, LAYER_S) == "s":
+                act("n%d" % m, vw("nn", SEG * m, SEG * m + A), vw("key"), ACT.Abs, bias=vw("nbs", m, m + 1), scale=1024.0)
             else:
-                for j, (lo, hi, at, st) in enumerate(((0, 256, 0, 1), (256, 384, 256, 2), (384, 448, 512, 4))):
-                    o = HW * m + at
-                    move("v" if w[0] == "h" else "s", T.ht[:, o:o + st * (hi - lo):st], bank(4 + m, lo, hi), "ps%d" % (4 + m), "h%d.%d" % (m, j), 0.03125)
-        cp(T.fo[:], T.jf[:, 223:12 * 224:224], toks("jf%d", range(12)), "fo")
-        for t in (0, 1, 2, 3):
-            move("vvss"[t], T.vt[:, t:4 * K:4], T.ht[:, HW * t:HW * (t + 1)].indirect(T.fo[:]), "h%d.0 h%d.1 h%d.2 fo" % (t, t, t), "vt%d" % t)
-        qz(T.rq[:, a:b], T.rsc[:, a:b], T.vt[:], "vt0 vt1 vt2 vt3", "rq%d" % r)
-        ship(before, T.rq, T.rsc, T.bq, T.bs, r, T.sem["ab%d" % r], "rq%d" % r)
-
+                ts("n%d" % m, vw("nn", SEG * m, SEG * m + A), vw("key"), vw("nb", m, m + 1), 1024.0, ALU.not_equal, ALU.mult)
         if r == 0:
-            qz(T.ecq[:], T.ecs[:], T.ec[:], "ec0 ec1 ec2 ec3", "ecq")
-            move("s", T.eh[:], T.et[:], "et0 et1", "eh", 0.25)
-            ts(T.own[:], T.i16[:], Q, None, ALU.add, None, "i16 q", "own")
-            ts(T.ownm[:], T.i16[:], Q, -512.0, ALU.add, ALU.add, "i16 q", "ownm")
-        ts(T.u1[:], T.rk[:], float(K), None, ALU.is_lt, None, "rk0 rk1 rk2", "u1")
-        ts(T.lw[:], T.mx2[:], 20, 3, ALU.arith_shift_right, ALU.bitwise_and, "mx20 mx21", "lw")
-        tt(T.u2[:], T.rk[:], T.ownm[:], ALU.subtract, "rk0 rk1 rk2 ownm", "u2")
+            for k in range(JG):
+                cp("en%d" % k, vw("en", SEG * k, SEG * (k + 1)), vw("en", 0, SEG) if k else vw("en0"))
+        for k in range(12 // JG):
+            lo, hi = SEG * JG * k, SEG * JG * (k + 1)
+            scan("j%d" % k, vw("jf", lo, hi, -1), vw("nn", lo, hi, -1), vw("en", 0, SEG * JG, -1), 0.0, ALU.min, ALU.max)
+        ts("fo", vw("fo"), vw("jf", 0, 12 * SEG, SEG), 0.0, None, ALU.add)
+        for t in range(4):
+            move("vt%d" % t, on("vt%d" % t, LAYER_S), vw("vt", t, 4 * K, 4), by(vw("ht", HW * t, HW * t + A + 1), vw("fo")))
+        qz("qv", vw("rq", a, b), vw("rsc", a, b), vw("vt"))
+        ship(before, "rq", "rsc", "bq", "bs", r, T.sem["ab%d" % r])
+        arrange(v=LAYER_V, s=LAYER_S)
+
+        rk = vw("cx", 15, 512, 16)
+        if r == 0:
+            move("", "s", vw("eh"), vw("et"), 0.25)
+            ts("", vw("own"), vw("i16"), Q, float(OWN), ALU.add, ALU.add)
+            ts("", vw("ownm"), vw("i16"), Q, OWN - 1024.0, ALU.add, ALU.add)
+        ts("", vw("u1"), rk, K - 1024.0, None, ALU.is_lt)
+        ts("", vw("lw"), vw("mx2"), 20, 3, ALU.arith_shift_right, ALU.bitwise_and)
+        tt("", vw("u2"), rk, vw("ownm"), ALU.subtract)
         for i in range(4 if r < R - 1 else 1):
-            tt(T.lt[:, i:112:4], T.lv[:, i:112:4], T.lw[:], ALU.subtract, "lv lw", "lt%d" % i)
-        tt(T.u3[:], T.u1[:], T.u2[:], ALU.mult, "u1 u2", "u3")
+            tt("", vw("lt", i, 112, 4), vw("lv", i, 112, 4), vw("lw"), ALU.subtract)
+        tt("", vw("u3"), vw("u1"), vw("u2"), ALU.mult)
         if r < R - 1:
-            ts(T.lt[:], T.lt[:], 3.0, None, ALU.add, None, "lt0 lt1 lt2 lt3", "lt0 lt1 lt2 lt3")
+            ts("", vw("lt"), vw("lt"), 3.0, None, ALU.add)
         else:
-            ts(T.ci[:], T.lt[:, 0:112:4], 4.0, None, ALU.add, None, "lt0", "ci")
-        tt(T.u4[:], T.u3[:], T.own[:], ALU.add, "u3 own", "u4")
+            ts("", vw("ci"), vw("lt", 0, 112, 4), 4.0, None, ALU.add)
+        tt("", vw("u4"), vw("u3"), vw("own"), ALU.add)
         if r < R - 1:
-            ts(T.lv[:], T.lt[:], 3, None, ALU.bitwise_and, None, "lt0 lt1 lt2 lt3", "lv")
+            ts("", vw("lv"), vw("lt"), 3, None, ALU.bitwise_and)
         else:
-            ts(T.cj[:], T.ci[:], 3, None, ALU.bitwise_and, None, "ci", "cj")
-            ms(T.cw[:, 28:32], 0.0, "cw1")
-        cp(T.uo[:], T.u4[:], "u4", "uo")
+            ts("", vw("cj"), vw("ci"), 3, None, ALU.bitwise_and)
+            ms("", vw("cw", 28, 32), 0.0)
+        cp("", vw("uo"), vw("u4"))
         if r < R - 1:
-            ts(T.wf[:], T.lv[:], float(2 ** 20), None, ALU.mult, None, "lv", "wf")
-            if r == 1:
-                qz(T.vq[:], T.vs[:], T.vb[:], "vb", "vq")
-            tt(T.wp[:], T.wf[:], T.pay[:], ALU.add, "wf pay", "wp")
+            ts("", vw("wf"), vw("lv"), float(2 ** 20), None, ALU.mult)
         else:
-            cp(T.cw[:, 0:28], T.cj[:], "cj", "cw0")
-            op("v", lambda: V.transpose(T.cwt[:], T.cw[:]), "cw0 cw1", "cwt")
+            cp("", vw("cw", 0, 28), vw("cj"))
+            op("", "v", lambda: V.transpose(T.cwt[:], T.cw[:]), (vw("cw"),), (vw("cwt"),))
             for gr in range(8):
                 p0, c0 = 32 * (gr // 2), 16 * (gr % 2)
-                dma("y", T.ow[gr:gr + 1, :], T.cwt[p0:p0 + 28, c0:c0 + 16], "stw", "cwt", "")
+                dma("y", T.ow[gr:gr + 1, :], T.cwt[p0:p0 + 28, c0:c0 + 16], "stw", (vw("cwt"),))
+        arrange()
 
         for t in range(4):
-            mm(4 + t, K, T.ecq[:, 128 * t:128 * (t + 1)], T.ecs[:, 128 * t:128 * (t + 1)], T.bq[:, a:b], T.bs[:, a:b], "ecq",
-               ext=(T.sem["ab%d" % r], n_from_after) if t == 0 else None)
-        for t in range(4):
-            tt(T.ph[:, PL * t + C:PL * (t + 1)], bank(4 + t, 0, K), T.eh[:, t:4 * K:4], ALU.add, "ps%d eh" % (4 + t), "pi_%d" % t)
-
-        def renew(eng, t, h):
-            move(eng, T.xa[:, 1024 * h + t:1024 * (h + 1):4], T.ph[:, PL * t:PL * (t + 1)].indirect(T.uo[:, 16 * h:16 * (h + 1)]),
-                 "po%d pi_%d uo" % (t, t), "x%d" % (4 * h + t), 2.0)
-
-        for eng, t, h in (("s", 0, 0), ("s", 1, 0), ("v", 2, 0), ("v", 3, 0), ("s", 0, 1), ("s", 1, 1), ("s", 2, 1)):
-            renew(eng, t, h)
+            mm("", 4 + t, "ebq", "ebs", 128 * t, "bq", "bs", a, b, ext=(T.sem["ab%d" % r], n_from_after) if t == 0 else None)
+            tt("ad%d" % t, vw("ph", PL * t, PL * t + K), bank(4 + t, 0, K), vw("eh", t, 4 * K, 4), ALU.add)
+        for h in range(2):
+            for t in range(4):
+                w = "rn%d%d" % (t, h)
+                move(w, on(w, RANK_S), vw("xa", 1024 * h + t, 1024 * (h + 1), 4), by(vw("ph", PL * t, PL * (t + 1)), vw("uo", 16 * h, 16 * (h + 1))), 2.0)
         q_half(0)
-        renew("v", 3, 1)
-        q_half(1)
 
-    mm(0, 256, T.vq[:], T.vs[:], T.xq[:, 0:256], T.xs[:, 0:256], "vq xq0")
-    mm(1, 256, T.vq[:], T.vs[:], T.xq[:, 256:512], T.xs[:, 256:512], "vq xq1")
-    dma("y", T.oc[:, 0:1024], T.xq[:, 0:256].bitcast(dt.uint8), "st", "xq0", "")
-    move("s", T.yo[:, 0:256], bank(0, 0, 256), "ps0", "yo0")
-    move("v", T.yo[:, 256:512], bank(1, 0, 256), "ps1", "yo1")
-    dma("s", T.y[:, 0:256], T.yo[:, 0:256], "st", "yo0", "")
-    dma("y", T.oc[:, 1024:2048], T.xq[:, 256:512].bitcast(dt.uint8), "st", "xq1", "")
+    q_half(1)
+    arrange(v=RANK_V, s=RANK_S)
+    for h in range(2):
+        mm("", h, "vq", "vs", 0, "xq", "xs", 256 * h, 256 * (h + 1))
+    dma("y", T.oc[:, 0:1024], T.xq[:, 0:256].bitcast(dt.uint8), "st", (vw("xq", 0, 256),))
+    move("", "s", vw("yo", 0, 256), bank(0, 0, 256))
+    move("", "v", vw("yo", 256, 512), bank(1, 0, 256))
+    dma("s", T.y[:, 0:256], T.yo[:, 0:256], "st", (vw("yo", 0, 256),))
+    dma("y", T.oc[:, 1024:2048], T.xq[:, 256:512].bitcast(dt.uint8), "st", (vw("xq", 256, 512),))
     for k in range(4):
-        dma("s", T.osc[4 * k:4 * k + 4, :], T.xs[32 * k:32 * k + 4, :], "st", "xq0 xq1", "")
-    dma("y", T.y[:, 256:512], T.yo[:, 256:512], "st", "yo1", "")
+        dma("s", T.osc[4 * k:4 * k + 4, :], T.xs[32 * k:32 * k + 4, :], "st", (vw("xs"),))
+    dma("y", T.y[:, 256:512], T.yo[:, 256:512], "st", (vw("yo", 256, 512),))
+    arrange()
 
-    writer, readers, known, seq = {}, {}, {e: {} for e in queue}, {e: 0 for e in queue}
+    seen = {}
     for n, o in enumerate(ops):
-        e = o["e"]
         deps = set()
-        for t in o["r"]:
-            if t in writer:
-                deps.add(writer[t])
-            if t.startswith("ps"):
-                deps.update(d for d in readers.get(t, ()) if ops[d]["e"] != e)
-        for t in o["w"]:
-            if t in writer and not o["acc"]:
-                deps.add(writer[t])
-            deps.update(readers.get(t, ()))
-        for t in o["r"]:
-            readers.setdefault(t, []).append(n)
-        for t in o["w"]:
-            writer[t] = n
-            readers[t] = []
-        deps.discard(n)
-        waits = []
-        for d in sorted(deps, reverse=True):
+        for wrote, views in ((False, o["r"]), (True, o["w"])):
+            for name, cols in views:
+                for c2, d, w2 in seen.get(name, ()):
+                    if c2 & cols and d != n and (w2 or wrote or (name == "ps" and ops[d]["e"] != o["e"])) and not (o["acc"] and wrote and ops[d]["e"] == "t"):
+                        deps.add(d)
+        for name, cols in o["r"]:
+            seen.setdefault(name, []).append((cols, n, False))
+        for name, cols in o["w"]:
+            seen[name] = [x for x in seen.get(name, ()) if x[0] & ~cols] + [(cols, n, True)]
+        o["deps"] = deps
+    known, seq, nxt, done = {e: {} for e in queue}, {e: 0 for e in queue}, {e: 0 for e in queue}, []
+    while len(done) < len(ops):
+        ready = [e for e in queue if nxt[e] < len(issue[e]) and all("clock" in ops[d] for d in ops[issue[e][nxt[e]]]["deps"])]
+        e = ready[0]
+        n = issue[e][nxt[e]]
+        nxt[e] += 1
+        o = ops[n]
+        o["waits"] = []
+        for d in sorted(o["deps"], key=lambda d: -ops[d]["at"]):
             p = ops[d]
             if known[e].get(p["key"], 0) >= p["seq"]:
                 continue
-            waits.append(d)
+            o["waits"].append(d)
             p["sig"] = True
             for k2, v2 in p["clock"].items():
                 known[e][k2] = max(known[e].get(k2, 0), v2)
-        o["waits"] = waits
-        if o["dma"]:
-            o["key"], o["seq"] = "dma" + str(n), 1
-        elif o["plain"]:
-            o["key"], o["seq"] = "rem" + str(n), 1
+        if o["dma"] or o["plain"]:
+            o["key"], o["seq"] = n, 1
         else:
             seq[e] += 1
             o["key"], o["seq"] = e, seq[e]
         o["clock"] = dict(known[e])
         o["clock"][o["key"]] = o["seq"]
+        o["at"] = len(done)
+        done.append(n)
     count = {e: 0 for e in queue}
     stores = {"st": 0, "stw": 0}
-    for o in ops:
+    for n in done:
+        o = ops[n]
         e = o["e"]
         for d in o["waits"]:
             p = ops[d]

from concourse.mybir import dt, AluOpType, ActivationFunctionType

ALU = AluOpType
ACT = ActivationFunctionType

C, K, A, R = 512, 192, 448, 3
OWN = K + 16
PL = OWN + C
HW = 464
SEG, JG = A + 1, 3
BIG = 1.0e25
HOLD = float(2 ** 22)
DROP = -float(2 ** 24)
TW = [512, 448, 384, 384, 256, 256, 128, 128]
TQ = [512, 448, 384, 320, 256, 192, 128, 128]
TO = [sum(TW[:t]) for t in range(8)]
TN = sum(TW)
STAGE = ((256, 512, 2), (128, 256, 6), (0, 128, 3))
CHUNK = ((128, 256), (0, 128), (384, 512), (256, 384))
PART = ((0, 8), (8, 28))
LISTS = ((0, 8), (16, 36))
FLAGS = ((0, 16), (16, 32), (32, 64), (64, 96), (96, 112))
OWNS = ((0, 32), (32, 64), (64, 96), (96, 112))
MV = 24
EARLY = (15, 14, 13)
S_ROWS = EARLY + tuple(m for m in range(MV - 1, 0, -1) if m not in EARLY)
AHEAD = (13, 9)
RANK_S = "rn00 rn10 rn01 rn11 rn21"
RANK_V = ("ad0 ad1 ad2 ad3 rn20 rn30 rn31 qx0 qx1 mn0 mn1 fs0 fs1 mn2 mn3 d0 fs2 fs3 c31 d1 c30 c29 c28 c27 dg c26 c25 q0 c24 r31 r30 r29 q1 r28 r27 q2 "
          "r26 t1 r25 r24 q3 aw av0 q4 cx0 q5 av1 ru0 cx1 sc0 ru1 q6 av2 q7 sc1 cx2 ru2 sc2 lx eo et0 qe")
LAYER_V = ("ft1 fl1 fl4 of0 pi0 a1 of3 a2 of1 a3 a4 pi1 a5 of2 en0 b1 z00 b2 z10 b3 b4 z20 b5 z30 en1 en2 qz0 n0 n1 n2 z01 n3 z11 n4 z21 n5 z31 j0 qz1 j1 j2 j3 fo vt0 vt1 qv")
LAYER_S = "fl0 fl2 fl3 pi2 pi3 s00 s10 s20 s30 k0 k1 s01 s11 s21 s31 n6 n7 n8 n9 n10 n11 h00 h10 h20 h30 h01 h11 h21 h31 vt2 vt3"

BF, F32, I32, U16, U8, X4, F16 = "bfloat16", "float32", "int32", "uint16", "uint8", "float8_e4m3fn_x4", "float16"


def _sb(n, d):
    return ("sbuf", [128, n], d)


SCRATCH = {
    "xa": _sb(4 * C, BF), "ub": _sb(512, BF), "vb": _sb(512, BF),
    "uq": _sb(128, X4), "us": _sb(128, U8), "urq": _sb(128, X4), "urs": _sb(128, U8),
    "vq": _sb(128, X4), "vs": _sb(128, U8), "wq": _sb(512, X4), "wsp": _sb(512, U8),
    "xq": _sb(512, X4), "xs": _sb(512, U8), "cli": _sb(112, I32), "clu": _sb(112, U16),
    "ct": _sb(4 * TN, BF), "cq": _sb(TN, X4), "cs": _sb(TN, U8),
    "one": _sb(512, BF), "quar": _sb(512, BF), "bd1": _sb(512, BF), "bd": _sb(512, BF), "bdq": _sb(128, X4), "bds": _sb(128, U8),
    "eb": _sb(2048, BF), "ebq": _sb(512, X4), "ebs": _sb(512, U8),
    "pi": _sb(8, I32), "pf": _sb(16, F32), "r16": _sb(128, BF), "r16k": _sb(128, F32), "r4": _sb(64, BF), "e0": _sb(128, BF), "e64": _sb(384, BF),
    "i16": _sb(32, F32), "uoi": _sb(8, I32), "uou": _sb(8, U16), "i704": _sb(C + K, F32), "io4": _sb(512, BF),
    "m1": _sb(128, BF), "k1": _sb(128, BF), "rst": _sb(512, BF), "a16": _sb(512, BF), "a4": _sb(192, BF), "av": _sb(512, F32),
    "base": _sb(32, F32), "own": _sb(32, F32), "ownm": _sb(32, F32),
    "mn": _sb(512, F32), "fs": _sb(512, F32), "sg": _sb(8 * MV * (MV - 1), BF), "jr": _sb(256 * (32 - MV), BF),
    "rs": _sb(32, F32), "dg": _sb(512, BF), "t1": _sb(32, F32), "cx": _sb(512, F32),
    "rku": _sb(32, U16), "ls": _sb(512, BF), "lx": _sb(192, F16), "eo": _sb(48, U16),
    "et": _sb(4 * K, BF), "eh": _sb(4 * K, BF),
    "eq": _sb(R * K, X4), "es": _sb(R * K, U8), "gq": _sb(R * K, X4), "gs": _sb(R * K, U8),
    "rq": _sb(R * K, X4), "rsc": _sb(R * K, U8), "bq": _sb(R * K, X4), "bs": _sb(R * K, U8),
    "ft": _sb(PL, BF), "ph": _sb(4 * PL, BF), "lr": _sb(4 * A, F32), "lxs": _sb(4 * A, F32),
    "lc": _sb(112, F32), "ou": _sb(112, U16), "pt": _sb(112, F32), "pay": _sb(112, F32),
    "lv": _sb(112, I32), "lt": _sb(112, I32), "lw": _sb(28, I32), "wf": _sb(112, F32), "wp": _sb(112, F32),
    "gf": _sb(4 * A, BF), "fx": _sb(4 * A, BF), "val": _sb(112, F32), "dw": _sb(112, F32), "mx2": _sb(28, I32),
    "oti": _sb(56, I32), "otu": _sb(56, U16),
    "pr": _sb(PL, BF), "en0": _sb(SEG, F32), "en": _sb(JG * SEG, F16), "nn": _sb(12 * SEG, BF), "jf": _sb(12 * SEG, F16),
    "nb": _sb(12, BF), "nbs": _sb(12, F32), "key": _sb(A, BF), "g2": _sb(4 * A, BF), "zt": _sb(4 * A, BF),
    "zq": _sb(A, X4), "zs": _sb(A, U8), "fo": _sb(12, U16),
    "ht": _sb(4 * HW, BF), "vt": _sb(4 * K, BF),
    "u1": _sb(32, F32), "u2": _sb(32, F32), "u3": _sb(32, F32), "uo": _sb(32, U16), "u4": _sb(32, F32),
    "ci": _sb(28, I32), "cj": _sb(28, I32), "cw": _sb(32, F32), "cwt": _sb(32, F32), "yo": _sb(512, F32),
    "ps": ("psum", [128, 4096], F32),
}
SEMAPHORES = ["cv", "cs_", "ct_", "cg", "ldx0", "ldx1", "ldu", "ldc", "ldw", "lds", "ldv", "sent", "st", "stw"] + \
    ["ae%d" % r for r in range(R)] + ["ab%d" % r for r in range(R)]


def rank_program(g, core, T, topo):
    rank = T.rank_of(core)
    if rank is None:
        return
    n_ranks = len(T.cores)
    after, before = T.cores[(rank + 1) % n_ranks], T.cores[(rank - 1) % n_ranks]
    V, S, PE, SY = g.vector, g.scalar, g.tensor, g.sync
    queue = {"v": V, "s": S, "t": PE, "g": g, "y": SY}
    counter = {"v": T.sem["cv"], "s": T.sem["cs_"], "t": T.sem["ct_"], "g": T.sem["cg"]}

    def vw(name, lo=0, hi=None, step=1):
        return (name, lo, SCRATCH[name][1][1] if hi is None else hi, step)

    def by(window, offsets):
        return (window, offsets)

    def ap(x):
        if not isinstance(x, tuple):
            return x
        if len(x) == 2:
            return ap(x[0]).indirect(ap(x[1]))
        name, lo, hi, step = x
        if step < 0:
            return T[name][:, hi - 1:(lo - 1 if lo else None):step]
        return T[name][:, lo:hi:step]

    def touched(x):
        if not isinstance(x, tuple):
            return []
        if len(x) == 2:
            return touched(x[0])
        name, lo, hi, step = x
        if name == "ps":
            return [(name, 1 << (lo // 512))]
        step = abs(step)
        n = (hi - lo + step - 1) // step
        return [(name, (((1 << (step * n)) - 1) // ((1 << step) - 1)) << lo)]

    ops, issue, fresh = [], {e: [] for e in queue}, []

    def op(name, eng, fn, reads, writes, ext=None, dma=None, acc=False, plain=False):
        r = [t for x in reads for t in touched(x)] + [t for x in list(reads) + list(writes) if isinstance(x, tuple) and len(x) == 2 for t in touched(x[1])]
        w = [t for x in writes for t in touched(x)]
        fresh.append(len(ops))
        ops.append({"name": name, "e": eng, "fn": fn, "r": r, "w": w, "ext": ext, "dma": dma, "acc": acc, "plain": plain})

    def arrange(**orders):
        for e in queue:
            mine = [n for n in fresh if ops[n]["e"] == e]
            if e in orders:
                place = {w: i for i, w in enumerate(orders[e].split())}
                mine.sort(key=lambda n: place[ops[n]["name"]])
            issue[e].extend(mine)
        del fresh[:]

    def ts(name, out, in0, s1, s2, o0, o1=None):
        if o1 is None:
            op(name, "v", lambda: V.tensor_scalar(ap(out), ap(in0), ap(s1), None, o0), (in0, s1), (out,))
        else:
            op(name, "v", lambda: V.tensor_scalar(ap(out), ap(in0), ap(s1), ap(s2), o0, o1), (in0, s1, s2), (out,))

    def tt(name, out, a, b, o):
        op(name, "v", lambda: V.tensor_tensor(ap(out), ap(a), ap(b), o), (a, b), (out,))

    def cp(name, out, a):
        op(name, "v", lambda: V.tensor_copy(ap(out), ap(a)), (a,), (out,))

    def ms(name, out, c):
        op(name, "v", lambda: V.memset(ap(out), c), (), (out,))

    def scan(name, out, d0, d1, init, o0, o1):
        op(name, "v", lambda: V.tensor_tensor_scan(ap(out), ap(d0), ap(d1), init, o0, o1), (d0, d1), (out,))

    def qz(name, q, s, a):
        op(name, "v", lambda: V.quantize_mx(ap(q), ap(s), ap(a)), (a,), (q, s))

    def act(name, out, a, f, bias=None, scale=None, accum=None):
        kw = {}
        for k, x in (("bias", bias), ("scale", scale), ("accum_out", accum)):
            if x is not None:
                kw[k] = ap(x)
        op(name, "s", lambda: S.activation(ap(out), ap(a), f, **kw), (a, bias, scale), (out, accum))

    def move(name, eng, out, a, times=None):
        if eng == "s":
            act(name, out, a, ACT.Copy, scale=times)
        elif times is None:
            cp(name, out, a)
        else:
            ts(name, out, a, times, None, ALU.mult)

    def on(name, s_order):
        return "s" if name in s_order.split() else "v"

    def bank(b, lo, hi):
        return vw("ps", 512 * b + lo, 512 * b + hi)

    def mm(name, b, lq, ls_, at, rq, rs_, lo, hi, start=True, stop=True, ext=None):
        views = (vw(lq, at, at + 128), vw(ls_, at, at + 128), vw(rq, lo, hi), vw(rs_, lo, hi))
        op(name, "t", lambda: PE.matmul_mx(ap(bank(b, 0, hi - lo)), *[ap(x) for x in views], start, stop), views, (bank(b, 0, hi - lo),),
           ext=ext, acc=not start)

    def iota(out, pat, base, cm):
        if SCRATCH[out[0]][2] == I32:
            op("", "g", lambda: g.iota(ap(out), pat, base, cm), (), (out,))
        else:
            op("", "g", lambda: g.iota(ap(out), pat, base, cm, allow_small_or_imprecise_dtypes=True), (), (out,))

    def select(out, src, pat, cmp, base, cm):
        op("", "g", lambda: g.affine_select(ap(out), ap(src), pat, cmp, 0.0, base, cm), (src,), (out,))

    def unit(out, src, b):
        select(vw(out, 512 * b, 512 * (b + 1)), vw(src), [[1, 512]], ALU.is_equal, -b, -4)

    def dma(eng, out, a, sem, reads=(), writes=()):
        op("", eng, lambda: queue[eng].dma_start(out, a), reads, writes, dma=sem)

    sent = [0]

    def ship(dst, sq, ss, dq, ds, r, sem):
        rid, pid, _ = topo.addr(dst)
        m = topo.mask(core, dst)
        a, b = K * r, K * (r + 1)
        op("", "g", lambda: g.remote_dma(T[dq][:, a:b].bitcast(dt.uint8), T[sq][:, a:b].bitcast(dt.uint8), sem, T.sem.sent, pid, rid, m),
           (vw(sq, a, b),), (), plain=True)
        op("", "g", lambda: g.remote_dma(T[ds][:, a:b], T[ss][:, a:b], sem, T.sem.sent, pid, rid, m), (vw(ss, a, b),), (), plain=True)
        sent[0] += 2 * len(topo.engines(core, dst))

    n_from_before = 2 * len(topo.engines(before, core))
    n_from_after = 2 * len(topo.engines(after, core))

    def slot_view(m, lo, hi):
        t, b = ((32 - m) // 4, (32 - m) % 4) if m else (0, 0)
        o = 4 * TO[t] + b
        return vw("ct", o + 4 * lo, o + 4 * (hi - 1) + 1, 4)

    Q, Q4, T4, Q1, Q41, QH, QB, QE, QH4, QK = (vw("pf", i, i + 1) for i in range(10))

    def q_half(h):
        qz("qx%d" % h, vw("xq", 256 * h, 256 * (h + 1)), vw("xs", 256 * h, 256 * (h + 1)), vw("xa", 1024 * h, 1024 * (h + 1)))

    dma("s", T.ub[:], T.u[:], "ldu", (), (vw("ub"),))
    dma("y", T.cli[:], T.cl[:], "ldc", (), (vw("cli"),))
    dma("y", T.xa[:, 0:1024], T.x[:, 0:1024], "ldx0", (), (vw("xa", 0, 1024),))
    dma("s", T.xa[:, 1024:2048], T.x[:, 1024:2048], "ldx1", (), (vw("xa", 1024, 2048),))

    iota(vw("pi", 0, 1), [[0, 1]], 0, 1)
    iota(vw("r16"), [[0, 8], [1, 16]], 0, 0)
    iota(vw("uoi"), [[16, 8]], 0, 0)
    iota(vw("r16k"), [[0, 8], [8192, 16]], 0, 0)
    iota(vw("r4"), [[0, 16], [1, 4]], 0, 0)
    iota(vw("i16"), [[16, 32]], 0, 0)
    iota(vw("i704", 0, C), [[1, C]], OWN, 0)
    iota(vw("i704", C, C + K), [[1, K]], 0, 0)
    ms("", vw("one"), 1.0)
    select(vw("rst"), vw("one"), [[0, 32], [1, 16]], ALU.is_gt, 0, 0)
    select(vw("bd1"), vw("one"), [[16, 8], [0, 64]], ALU.is_ge, 15, -1)
    select(vw("bd"), vw("bd1"), [[-16, 8], [0, 64]], ALU.is_ge, 0, 1)
    iota(vw("io4"), [[1, 512]], -256, 0)
    iota(vw("lv"), [[0, 28], [-1, 4]], 3, 0)
    for t in range(8):
        lo = 16 * (29 - 4 * t)
        move("", "s", vw("ct", 4 * (TO[t] + lo), 4 * (TO[t] + TW[t])), vw("one", 0, 4 * (TW[t] - lo)), 0.0)
    ts("", vw("pi", 1, 2), vw("pi", 0, 1), 15, None, ALU.bitwise_and)
    ts("", vw("pi", 2, 3), vw("pi", 0, 1), 2, 3, ALU.arith_shift_right, ALU.bitwise_and)
    ts("", vw("pi", 3, 4), vw("pi", 0, 1), 3, None, ALU.bitwise_and)
    ts("", vw("k1"), vw("r16"), 0.5, 2 * BIG, ALU.subtract, ALU.mult)
    cp("", vw("pf", 0, 3), vw("pi", 1, 4))
    cp("", vw("uou"), vw("uoi"))
    ts("", vw("e0"), vw("r16"), Q, None, ALU.is_equal)
    ts("", QK, Q, 8192.0, -4096.0, ALU.mult, ALU.add)
    ts("", QB, Q, 4095.0, 15.0 - 15 * 4096.0 - 1024.0, ALU.mult, ALU.add)
    ts("", vw("m1"), vw("e0"), 2 * BIG, -BIG, ALU.mult, ALU.add)
    ts("", Q41, Q4, 1.0, None, ALU.add)
    ts("", Q1, Q, 1.0, None, ALU.add)
    ts("", QH4, Q4, 3.0, -4096.0, ALU.is_lt, ALU.mult)
    ts("", QH, Q, 15.0, -HOLD, ALU.is_lt, ALU.mult)
    ts("", vw("av", 0, 128), vw("r16k"), QK, 4096.0, ALU.subtract, ALU.min)
    ms("", vw("rs", 0, 1), 0.0)
    ts("", vw("e64", 0, 64), vw("r4"), Q4, -4096.0, ALU.is_equal, ALU.mult)
    ts("", vw("e64", 64, 128), vw("r4"), Q41, 1024.0, ALU.is_equal, ALU.mult)
    ts("", vw("e64", 128, 256), vw("e0"), DROP, None, ALU.mult)
    ts("", vw("e64", 256, 384), vw("r16"), Q1, HOLD, ALU.is_equal, ALU.mult)
    ts("", vw("base", 0, MV), vw("i16", 0, MV), QB, None, ALU.add)
    ts("", vw("base", MV, 32), vw("i16", MV, 32), QB, -248.0, ALU.add, ALU.add)
    tt("", vw("a4", 0, 64), vw("e64", 0, 64), vw("e64", 64, 128), ALU.add)
    ts("", QE, T4, QH4, 1024.0, ALU.add, ALU.add)
    tt("", vw("a16", 0, 128), vw("e64", 128, 256), vw("e64", 256, 384), ALU.add)
    for name, n, end in (("av", 128, 512), ("a4", 64, K), ("a16", 128, 512)):
        for at in range(n, end, n):
            move("", "s", vw(name, at, at + n), vw(name, 0, n))
    op("", "g", lambda: g.affine_select(T.quar[:], T.one[:], [[0, 512]], ALU.is_gt, 0.25, 0, 0), (vw("one"),), (vw("quar"),))
    cp("", vw("clu"), vw("cli"))
    qz("", vw("uq"), vw("us"), vw("ub"))
    op("", "v", lambda: V.tensor_copy(T.urq[:].bitcast(dt.uint32), T.uq[:].bitcast(dt.uint32).indirect(T.uou[:])), (vw("uq"), vw("uou")), (vw("urq"),))
    cp("", vw("urs"), by(vw("us"), vw("uou")))
    dma("y", T.wq[:].bitcast(dt.uint8), T.wc[:], "ldw", (vw("urs"),), (vw("wq"),))
    dma("y", T.wsp[:], T.ws[:], "lds", (), (vw("wsp"),))
    dma("y", T.vb[:], T.v[:], "ldv", (), (vw("vb"),))
    q_half(0)

    def clause_rows(name, lo, hi):
        move(name, "s", vw("lr", 16 * lo, 16 * hi), by(vw("i704"), vw("clu", lo, hi)))

    clause_rows("", 0, 40)
    for b in range(4):
        unit("eb", "quar", b)
    iota(vw("en0"), [[1, SEG]], 0, 0)
    iota(vw("ft", K, OWN), [[0, 16]], 0, 0)
    for t in range(4):
        iota(vw("ph", PL * t + K, PL * t + OWN), [[0, 16]], 0, 0)
    iota(vw("ht", A, 4 * HW, HW), [[0, 4]], 0, 0)
    arrange()

    def words(between):
        tt("", vw("wp"), vw("wf"), vw("pay"), ALU.add)
        between()
        for i in range(1, 4):
            tt("", vw("dw", i, 112, 4), vw("wp", i - 1, 112, 4), vw("wp", i, 112, 4), ALU.subtract)

    def clause_tables():
        for i in range(4):
            scan("", vw("lxs", A * i, A * (i + 1)), vw("a16", 0, A), vw("lr", i, 4 * A, 4), 0.0, ALU.add, ALU.max)
            if i:
                ts("", vw("lc", i - 1, 112, 4), vw("lxs", A * (i - 1) + 15, A * i, 16), QH, None, ALU.add)
        ts("", vw("wf"), vw("lv"), float(2 ** 20), None, ALU.mult)
        ts("", vw("nb"), vw("i16", 0, 12), Q, None, ALU.add)
        ts("", vw("nbs"), vw("i16", 0, 12), Q, -1024.0, ALU.add, ALU.mult)
        ts("", vw("lc", 3, 112, 4), vw("lxs", A * 3 + 15, A * 4, 16), QH, None, ALU.add)
        for i in (3, 0, 1, 2):
            ts("", vw("pt", i, 112, 4), vw("lc", (i + 1) % 4, 112, 4), 1024.0, QH, ALU.mult, ALU.add)
        cp("", vw("ou"), vw("lc"))
        ms("", vw("nn", A, 12 * SEG, SEG), 0.0)
        ms("", vw("dw", 0, 112, 4), 2 * DROP)
        tt("", vw("pay"), vw("pt"), vw("lc"), ALU.add)
        words(lambda: qz("", vw("ebq"), vw("ebs"), vw("eb")))

    for r in range(R):
        a, b = K * r, K * (r + 1)
        for bk in (4, 5):
            mm("", bk, "urq", "urs", 0, "xq", "xs", 0, 256)
        q_half(1)
        for bk in (0, 1):
            mm("", bk, "urq", "urs", 0, "xq", "xs", 0, 512)
        if r == 0:
            qz("q0", vw("bdq"), vw("bds"), vw("bd"))

        for h, (lo, hi) in enumerate(CHUNK):
            tt("mn%d" % h, vw("mn", lo, hi), bank(4 if hi <= 256 else 0, lo, hi), vw("m1"), ALU.min)
            scan("fs%d" % h, vw("fs", lo, hi), vw("k1"), vw("mn", lo, hi), -BIG, ALU.min, ALU.max)
        for h, (lo, hi) in enumerate(((0, 256), (256, 512))):
            tt("d%d" % h, slot_view(0, lo, hi), bank(0 if h else 4, lo, hi), vw("fs", lo, hi), ALU.is_le)
        scan("dg", vw("dg"), vw("rst"), slot_view(0, 0, 512), 0.0, ALU.mult, ALU.add)
        tt("t1", vw("t1"), vw("base"), vw("dg", 15, 512, 16), ALU.subtract)
        for m in range(31, 0, -1):
            col = vw("fs", 16 * m + 15, 16 * m + 16)
            if m in S_ROWS:
                sg = vw("sg", 8 * m * (m - 1), 8 * m * (m + 1))
                act("g%d" % m, sg, bank(5 if m in EARLY else 1, 0, 16 * m), ACT.Sign, bias=col, scale=-1.0)
                act("p%d" % m, slot_view(m, 0, 16 * m), sg, ACT.Relu, accum=vw("rs", m, m + 1))
            else:
                ts("c%d" % m, slot_view(m, 0, 16 * m), bank(4 if m in EARLY else 0, 0, 16 * m), col, None, ALU.is_lt)
                scan("r%d" % m, vw("jr", 256 * (m - MV + 1) - 8 * m, 256 * (m - MV + 1)), slot_view(m, 0, 8 * m), slot_view(m, 8 * m, 16 * m), -248.0, ALU.add, ALU.add)
        tiles = [int(w[1:]) for w in RANK_V.split() if w[0] == "q" and w[1:].isdigit()]
        for t in tiles:
            o, n = TO[t], (TQ if r else TW)[t]
            qz("q%d" % t, vw("cq", o, o + n), vw("cs", o, o + n), vw("ct", 4 * o, 4 * (o + n)))
            for lo, hi, bk in STAGE:
                adding = [u for u in tiles if TW[u] > lo]
                if t in adding:
                    mm("", bk, "bdq", "bds", 0, "cq", "cs", o + lo, o + min(hi, TW[t]), start=t == adding[0], stop=t == adding[-1])
        tt("aw", vw("av", 16 * MV + 15, 512, 16), vw("t1", MV, 32), vw("jr", 255, 256 * (32 - MV), 256), ALU.subtract)
        for k, (lo, hi, bk) in enumerate(STAGE):
            m0, m1 = lo // 16, hi // 16
            tt("av%d" % k, vw("av", lo + 15, 16 * min(m1, MV), 16), vw("t1", m0, min(m1, MV)), vw("rs", m0, min(m1, MV)), ALU.subtract)
            scan("cx%d" % k, vw("cx", lo, hi), bank(bk, 0, hi - lo), vw("av", lo, hi), -1.0, ALU.max, ALU.add)
            ts("ru%d" % k, vw("rku", m0, m1), vw("cx", lo + 15, hi, 16), 1024.0, None, ALU.add)
            cp("sc%d" % k, by(vw("ls"), vw("rku", m0, m1)), vw("io4", lo, hi))
        if r == 0:
            clause_rows("late", 40, 112)
        scan("lx", vw("lx"), vw("a4"), vw("ls", 0, K), 0.0, ALU.add, ALU.max)
        ts("eo", vw("eo"), vw("lx", 3, K, 4), 4.0, QE, ALU.mult, ALU.add)
        move("et1", "s", vw("et", 384, 768), by(vw("xa"), vw("eo", 24, 48)))
        move("et0", "v", vw("et", 0, 384), by(vw("xa"), vw("eo", 0, 24)))
        qz("qe", vw("eq", a, b), vw("es", a, b), vw("et"))
        ship(after, "eq", "es", "gq", "gs", r, T.sem["ae%d" % r])
        rows, todo = [], list(S_ROWS)
        for i, m in enumerate(S_ROWS):
            while todo and len(S_ROWS) - len(todo) <= i + (1 if m >= AHEAD[0] else 2 if m >= AHEAD[1] else 4):
                rows.append("g%d" % todo.pop(0))
            rows.append("p%d" % m)
        arrange(v=RANK_V, s=RANK_S + " " + " ".join(rows) + " late et1")

        if r == 0:
            iota(vw("pr"), [[1, PL]], 0, 0)
        if r == 0:
            act("", vw("ft", OWN, PL), bank(1, 0, 512), ACT.Sign)
        else:
            words(lambda: ts("", vw("ft", OWN, PL), bank(0, 0, 512), 0.0, None, ALU.is_gt))
        for t in range(4):
            move("", "s" if t < 3 or r == 0 else "v", vw("ph", PL * t + OWN, PL * (t + 1)), vw("xa", t, 2048, 4), 0.5)
        if r == 0:
            clause_tables()
        else:
            move("", "v", vw("eh"), vw("et"), 0.25)
        if r == 1:
            qz("", vw("vq"), vw("vs"), vw("vb"))
        arrange()

        mm("", 2, "urq", "urs", 0, "gq", "gs", a, b, ext=(T.sem["ae%d" % r], n_from_before))
        for t in range(4):
            mm("", 4 + t, "ebq", "ebs", 128 * t, "gq", "gs", a, b)
        ts("ft1", vw("ft", 0, K), bank(2, 0, K), 0.0, None, ALU.is_gt)
        for k, (lo, hi) in enumerate(FLAGS):
            named = by(vw("ft"), vw("ou", lo, hi))
            if on("fl%d" % k, LAYER_S) == "s":
                act("fl%d" % k, vw("gf", 16 * lo, 16 * hi), named, ACT.Relu, scale=HOLD)
            else:
                ts("fl%d" % k, vw("gf", 16 * lo, 16 * hi), named, 0.0, HOLD, ALU.max, ALU.mult)
        for k, (lo, hi) in enumerate(OWNS):
            scan("of%d" % k, vw("fx", 16 * lo, 16 * hi), vw("a16", 0, 16 * (hi - lo)), vw("gf", 16 * lo, 16 * hi), 0.0, ALU.add, ALU.max)
        for h, (c0, c1) in enumerate(PART):
            w, (o1, o2) = "ab"[h], LISTS[h]
            scan(w + "1", vw("val", 4 * c0, 4 * c1), vw("dw", 4 * c0, 4 * c1), vw("fx", 64 * c0 + 15, 64 * c1, 16), 0.0, ALU.add, ALU.max)
            tt(w + "2", vw("mx2", c0, c1), vw("val", 4 * c0 + 3, 4 * c1, 4), vw("wp", 4 * c0 + 3, 4 * c1, 4), ALU.add)
            ts(w + "3", vw("oti", o2, o2 + c1 - c0), vw("mx2", c0, c1), 10, 1023, ALU.arith_shift_right, ALU.bitwise_and)
            ts(w + "4", vw("oti", o1, o1 + c1 - c0), vw("mx2", c0, c1), 1023, None, ALU.bitwise_and)
            cp(w + "5", vw("otu", 2 * c0, 2 * c1), vw("oti", 2 * c0, 2 * c1))
        for t in range(4):
            move("pi%d" % t, on("pi%d" % t, LAYER_S), vw("ph", PL * t, PL * t + K), bank(4 + t, 0, K), 2.0)

        for h, (c0, c1) in enumerate(PART):
            lo, hi = 16 * c0, 16 * c1
            one, two = (vw("otu", o, o + c1 - c0) for o in LISTS[h])
            move("k%d" % h, on("k%d" % h, LAYER_S), vw("key", lo, hi), by(vw("pr"), one))
            for t in range(4):
                plane, w = vw("ph", PL * t, PL * (t + 1)), "%d%d" % (t, h)
                move("s" + w, on("s" + w, LAYER_S), vw("g2", A * t + lo, A * t + hi), by(plane, two))
                tt("z" + w, vw("zt", 4 * lo + t, 4 * hi, 4), by(plane, one), vw("g2", A * t + lo, A * t + hi), ALU.add)
            qz("qz%d" % h, vw("zq", lo, hi), vw("zs", lo, hi), vw("zt", 4 * lo, 4 * hi))
            for t in range(4):
                bk, w = 4 * (1 - h) + t, "h%d%d" % (t, h)
                mm("", bk, "wq", "wsp", 128 * t, "zq", "zs", lo, hi)
                move(w, on(w, LAYER_S), vw("ht", HW * t + lo, HW * t + hi), bank(bk, 0, hi - lo), 0.03125)
        for m in range(12):
            if on("n%d" % m, LAYER_S) == "s":
                act("n%d" % m, vw("nn", SEG * m, SEG * m + A), vw("key"), ACT.Abs, bias=vw("nbs", m, m + 1), scale=1024.0)
            else:
                ts("n%d" % m, vw("nn", SEG * m, SEG * m + A), vw("key"), vw("nb", m, m + 1), 1024.0, ALU.not_equal, ALU.mult)
        if r == 0:
            for k in range(JG):
                cp("en%d" % k, vw("en", SEG * k, SEG * (k + 1)), vw("en", 0, SEG) if k else vw("en0"))
        for k in range(12 // JG):
            lo, hi = SEG * JG * k, SEG * JG * (k + 1)
            scan("j%d" % k, vw("jf", lo, hi, -1), vw("nn", lo, hi, -1), vw("en", 0, SEG * JG, -1), 0.0, ALU.min, ALU.max)
        ts("fo", vw("fo"), vw("jf", 0, 12 * SEG, SEG), 0.0, None, ALU.add)
        for t in range(4):
            move("vt%d" % t, on("vt%d" % t, LAYER_S), vw("vt", t, 4 * K, 4), by(vw("ht", HW * t, HW * t + A + 1), vw("fo")))
        qz("qv", vw("rq", a, b), vw("rsc", a, b), vw("vt"))
        ship(before, "rq", "rsc", "bq", "bs", r, T.sem["ab%d" % r])
        arrange(v=LAYER_V, s=LAYER_S)

        rk = vw("cx", 15, 512, 16)
        if r == 0:
            move("", "s", vw("eh"), vw("et"), 0.25)
            ts("", vw("own"), vw("i16"), Q, float(OWN), ALU.add, ALU.add)
            ts("", vw("ownm"), vw("i16"), Q, OWN - 1024.0, ALU.add, ALU.add)
        ts("", vw("u1"), rk, K - 1024.0, None, ALU.is_lt)
        ts("", vw("lw"), vw("mx2"), 20, 3, ALU.arith_shift_right, ALU.bitwise_and)
        tt("", vw("u2"), rk, vw("ownm"), ALU.subtract)
        for i in range(4 if r < R - 1 else 1):
            tt("", vw("lt", i, 112, 4), vw("lv", i, 112, 4), vw("lw"), ALU.subtract)
        tt("", vw("u3"), vw("u1"), vw("u2"), ALU.mult)
        if r < R - 1:
            ts("", vw("lt"), vw("lt"), 3.0, None, ALU.add)
        else:
            ts("", vw("ci"), vw("lt", 0, 112, 4), 4.0, None, ALU.add)
        tt("", vw("u4"), vw("u3"), vw("own"), ALU.add)
        if r < R - 1:
            ts("", vw("lv"), vw("lt"), 3, None, ALU.bitwise_and)
        else:
            ts("", vw("cj"), vw("ci"), 3, None, ALU.bitwise_and)
            ms("", vw("cw", 28, 32), 0.0)
        cp("", vw("uo"), vw("u4"))
        if r < R - 1:
            ts("", vw("wf"), vw("lv"), float(2 ** 20), None, ALU.mult)
        else:
            cp("", vw("cw", 0, 28), vw("cj"))
            op("", "v", lambda: V.transpose(T.cwt[:], T.cw[:]), (vw("cw"),), (vw("cwt"),))
            for gr in range(8):
                p0, c0 = 32 * (gr // 2), 16 * (gr % 2)
                dma("y", T.ow[gr:gr + 1, :], T.cwt[p0:p0 + 28, c0:c0 + 16], "stw", (vw("cwt"),))
        arrange()

        for t in range(4):
            mm("", 4 + t, "ebq", "ebs", 128 * t, "bq", "bs", a, b, ext=(T.sem["ab%d" % r], n_from_after) if t == 0 else None)
            tt("ad%d" % t, vw("ph", PL * t, PL * t + K), bank(4 + t, 0, K), vw("eh", t, 4 * K, 4), ALU.add)
        for h in range(2):
            for t in range(4):
                w = "rn%d%d" % (t, h)
                move(w, on(w, RANK_S), vw("xa", 1024 * h + t, 1024 * (h + 1), 4), by(vw("ph", PL * t, PL * (t + 1)), vw("uo", 16 * h, 16 * (h + 1))), 2.0)
        q_half(0)

    q_half(1)
    arrange(v=RANK_V, s=RANK_S)
    for h in range(2):
        mm("", h, "vq", "vs", 0, "xq", "xs", 256 * h, 256 * (h + 1))
    dma("y", T.oc[:, 0:1024], T.xq[:, 0:256].bitcast(dt.uint8), "st", (vw("xq", 0, 256),))
    move("", "s", vw("yo", 0, 256), bank(0, 0, 256))
    move("", "v", vw("yo", 256, 512), bank(1, 0, 256))
    dma("s", T.y[:, 0:256], T.yo[:, 0:256], "st", (vw("yo", 0, 256),))
    dma("y", T.oc[:, 1024:2048], T.xq[:, 256:512].bitcast(dt.uint8), "st", (vw("xq", 256, 512),))
    for k in range(4):
        dma("s", T.osc[4 * k:4 * k + 4, :], T.xs[32 * k:32 * k + 4, :], "st", (vw("xs"),))
    dma("y", T.y[:, 256:512], T.yo[:, 256:512], "st", (vw("yo", 256, 512),))
    arrange()

    seen = {}
    for n, o in enumerate(ops):
        deps = set()
        for wrote, views in ((False, o["r"]), (True, o["w"])):
            for name, cols in views:
                for c2, d, w2 in seen.get(name, ()):
                    if c2 & cols and d != n and (w2 or wrote or (name == "ps" and ops[d]["e"] != o["e"])) and not (o["acc"] and wrote and ops[d]["e"] == "t"):
                        deps.add(d)
        for name, cols in o["r"]:
            seen.setdefault(name, []).append((cols, n, False))
        for name, cols in o["w"]:
            seen[name] = [x for x in seen.get(name, ()) if x[0] & ~cols] + [(cols, n, True)]
        o["deps"] = deps
    known, seq, nxt, done = {e: {} for e in queue}, {e: 0 for e in queue}, {e: 0 for e in queue}, []
    while len(done) < len(ops):
        ready = [e for e in queue if nxt[e] < len(issue[e]) and all("clock" in ops[d] for d in ops[issue[e][nxt[e]]]["deps"])]
        e = ready[0]
        n = issue[e][nxt[e]]
        nxt[e] += 1
        o = ops[n]
        o["waits"] = []
        for d in sorted(o["deps"], key=lambda d: -ops[d]["at"]):
            p = ops[d]
            if known[e].get(p["key"], 0) >= p["seq"]:
                continue
            o["waits"].append(d)
            p["sig"] = True
            for k2, v2 in p["clock"].items():
                known[e][k2] = max(known[e].get(k2, 0), v2)
        if o["dma"] or o["plain"]:
            o["key"], o["seq"] = n, 1
        else:
            seq[e] += 1
            o["key"], o["seq"] = e, seq[e]
        o["clock"] = dict(known[e])
        o["clock"][o["key"]] = o["seq"]
        o["at"] = len(done)
        done.append(n)
    count = {e: 0 for e in queue}
    stores = {"st": 0, "stw": 0}
    for n in done:
        o = ops[n]
        e = o["e"]
        for d in o["waits"]:
            p = ops[d]
            if p["dma"]:
                queue[e].wait_ge(T.sem[p["dma"]], 16)
            else:
                queue[e].wait_ge(counter[p["e"]], p["cnt"])
        if o["ext"]:
            queue[e].wait_ge(o["ext"][0], o["ext"][1])
        ins = o["fn"]()
        if o["dma"]:
            ins.then_inc(T.sem[o["dma"]], 16)
            if o["dma"] in stores:
                stores[o["dma"]] += 16
        elif o.get("sig"):
            count[e] += 1
            o["cnt"] = count[e]
            ins.then_inc(counter[e], 1)
    g.wait_ge(T.sem.sent, sent[0])
    SY.wait_ge(T.sem.stw, stores["stw"])
    SY.wait_ge(T.sem.st, stores["st"])
